import numpy as np
import ml_dtypes


def mxq(x, axis, fmt="e4m3"):
    dtype, down = {"e4m3": (ml_dtypes.float8_e4m3fn, 7), "e5m2": (ml_dtypes.float8_e5m2, 14)}[fmt]
    v = np.moveaxis(np.asarray(x, np.float32).astype(ml_dtypes.bfloat16).astype(np.float64), axis, -1)
    blocks = v.reshape(v.shape[:-1] + (-1, 32))
    amax = np.abs(blocks).max(-1, keepdims=True)
    byte = np.maximum(np.where(amax > 0, np.frexp(amax)[1] - 1 + 127, 0) - down, 1)
    scale = np.exp2(byte - 127.0)
    codes = (blocks / scale).astype(np.float32).astype(dtype).astype(np.float64)
    return np.moveaxis((codes * scale).reshape(v.shape), -1, axis)


WIDE = False


def mx_kscale(k):
    if not WIDE:
        return np.ones(k)
    levels = np.array([10, -10, 5, -5, 0])
    if k % 512:
        return np.exp2(np.random.permutation(np.resize(levels, k // 32))).repeat(32)
    a = np.empty((k // 512, 16))
    for p in range(k // 512):
        a[p, :8] = np.random.permutation(np.resize(levels, 8))
        for g in range(8):
            far = levels[np.abs(levels - a[p, g]) >= 10]
            a[p, g + 8] = far[np.random.randint(len(far))]
    return np.exp2(a.ravel()).repeat(32)


def f64(x):
    return np.asarray(x).astype(np.float64)


def striped(idx):
    return np.tile(idx.reshape(-1, 16).T, (8, 1)).astype(np.uint16)


def unstriped(offs):
    return offs[:16].T.reshape(-1).astype(np.int64)


E2M1 = np.array([0.0, 0.5, 1.0, 1.5, 2.0, 3.0, 4.0, 6.0, -0.0, -0.5, -1.0, -1.5, -2.0, -3.0, -4.0, -6.0])


def pack_fp4(w):
    k, n = w.shape
    w = f64(np.asarray(w, np.float32).astype(ml_dtypes.bfloat16)).reshape(k // 32, 32, n)
    amax = np.abs(w).max(1)
    mant, ex = np.frexp(amax / 6.0)
    byte = np.clip(np.where(amax > 0, np.where(mant > 0.5, ex, ex - 1) + 127, 1), 1, 254)
    scaled = (w * np.exp2(127.0 - byte)[:, None, :]).reshape(k, n).astype(np.float32)
    c = np.ascontiguousarray(scaled.reshape(k // 512, 128, 4, n).transpose(0, 1, 3, 2)).astype(ml_dtypes.float4_e2m1fn).view(np.uint8) & 0xF
    words = (c[..., 0::2] | (c[..., 1::2] << 4)).reshape(k // 512, 128, 2 * n)
    return np.ascontiguousarray(words), np.ascontiguousarray(byte.astype(np.uint8).reshape(k // 512, 16, n))


def unpack_fp4(words, scales):
    g, _, n = scales.shape
    words = np.ascontiguousarray(words).reshape(g, 128, n, 2)
    nib = np.empty((g, 128, n, 4), np.uint8)
    nib[..., 0::2] = words & 0xF
    nib[..., 1::2] = words >> 4
    vals = E2M1[nib] * np.repeat(np.exp2(scales.astype(np.float64) - 127.0), 8, axis=1)[..., None]
    return vals.transpose(0, 1, 3, 2).reshape(g * 512, n)


def silu(v):
    return v / (1.0 + np.exp(-np.maximum(v, -700.0)))


K, T, S, N = 1024, 1024, 512, 256


def setup_inputs():
    n = np.random.standard_normal
    s = mx_kscale(K)[:, None]
    packed_w1 = pack_fp4(n((K, N)) / np.sqrt(K) / s)
    return {
        "xT": (n((K, T)) * s).astype(np.float32),
        "side": n((N, T)).astype(np.float32),
        "w1_words": packed_w1[0],
        "w1_scales": packed_w1[1],
        "offs": striped(np.random.permutation(T)[:S]),
    }


def reference(xT, side, w1_words, w1_scales, offs):
    xq = mxq(f64(xT)[:, unstriped(offs)], 0, "e4m3")
    y = unpack_fp4(w1_words, w1_scales).T @ xq
    g = f64(side)[:, unstriped(offs)]
    return y * silu(g)

@@ -1,0 +1,153 @@
+from contextlib import ExitStack
+
+import concourse.mybir as mybir
+
+K, T, S, N = 1024, 1024, 512, 256
+FLOPS = 2 * K * N * S
+
+F32 = mybir.dt.float32
+BF16 = mybir.dt.bfloat16
+I32 = mybir.dt.int32
+U32 = mybir.dt.uint32
+U16 = mybir.dt.uint16
+U8 = mybir.dt.uint8
+FP8X4 = mybir.dt.float8_e4m3fn_x4
+FP4X4 = mybir.dt.float4_e2m1fn_x4
+SILU = mybir.ActivationFunctionType.Silu
+MULT = mybir.AluOpType.mult
+
+P = 128
+PASSES = 2
+HALF = S // 2
+
+
+def tile_picked_sidegate_silu_l_kernel(tc, xT, side, w1_words, w1_scales, offs, out):
+    nc = tc.nc
+    with ExitStack() as ctx:
+        keep = ctx.enter_context(tc.tile_pool(name="keep", bufs=1))
+        psum = ctx.enter_context(tc.psum_pool(name="psum", bufs=1))
+
+        first, second, whole = slice(0, HALF), slice(HALF, S), slice(0, S)
+        offsets = keep.tile([P, S // 16], U16, name="offsets")
+        w_codes = keep.tile([P, PASSES, 2 * N], U8, name="w_codes", align_bytes=64)
+        w_scales = keep.tile([P, PASSES, N], U8, name="w_scales", align_bytes=64)
+        side_rows = [keep.tile([P, T], F32, name=f"side_rows{m}") for m in range(2)]
+        gate = [keep.tile([P, S], F32, name=f"gate{m}") for m in range(2)]
+        result = [keep.tile([P, S], F32, name=f"result{m}") for m in range(2)]
+        pairs = [keep.tile([P, T], U32, name=f"pairs{i}") for i in range(4)]
+        spans = [[whole], [first, second]]
+        picked = [[keep.tile([P, 2, cols.stop - cols.start], U32, name=f"picked{z}_{c}", align_bytes=64) for c, cols in enumerate(spans[z])] for z in range(PASSES)]
+        x_codes = [keep.tile([P, S], U32, name=f"x_codes{z}", align_bytes=64) for z in range(PASSES)]
+        x_scales = [keep.tile([P, S], U8, name=f"x_scales{z}", align_bytes=64) for z in range(PASSES)]
+        acc = [[psum.tile([P, P], F32, name=f"acc{m}_{g}") for g in range(4)] for m in range(2)]
+
+        pieces = [[[0,1024,672]],[[0,1024,672]],[[0,1024,640]],[[0,1024,352]]]
+        raw = [keep.tile([P, 2 * T + (2 * S - 16 if i == 2 else 0)], F32, name=f"raw{i}", align_bytes=64) for i in range(4)]
+        woven = [raw[2][:, 2 * T - 16 :].bitcast(U32), keep.tile([P, 2 * S], U32, name="woven1", align_bytes=64)[:]]
+
+
+        def offsets_of(cols):
+            return offsets[:, cols.start // 16 : cols.stop // 16]
+
+        def load_pair(i):
+            z, h = divmod(i, 2)
+            rows = xT[512 * z : 512 * (z + 1), :].rearrange("(p t) w -> p t w", t=4)
+            for n, (a, b, s) in enumerate(pieces[i]):
+                nc.sync.dma_start(out=raw[i][:, : 2 * T].rearrange("p (t w) -> p t w", t=2)[:, :, a:b], in_=rows[:, 2 * h : 2 * h + 2, a:b])
+
+        def load_scales():
+            for q in range(4):
+                nc.sync.dma_start(
+                    out=w_scales[32 * q : 32 * q + 4, :, :].bitcast(I32),
+                    in_=w1_scales[:, 4 * q : 4 * q + 4, :].rearrange("z r c -> r z c").bitcast(I32),
+                )
+
+        def load_side(m):
+            nc.sync.dma_start(out=side_rows[m][:], in_=side[P * m : P * (m + 1), :])
+
+        def load_codes():
+            nc.sync.dma_start(out=w_codes[:].bitcast(I32), in_=w1_words.rearrange("z p b -> p z b").bitcast(I32))
+
+        def cast_piece(i, n):
+            halves = pairs[i][:].bitcast(BF16).rearrange("p (w t) -> p w t", t=2)
+            a, b, s = pieces[i][n]
+            src = raw[i][:, : 2 * T].rearrange("p (t w) -> p w t", t=2)
+            if s < b:
+                nc.scalar.copy(halves[:, s:b, :], src[:, s:b, :])
+            if s > a:
+                nc.vector.tensor_copy(halves[:, a:s, :], src[:, a:s, :])
+
+        def gather_pair(i, c):
+            z, h = divmod(i, 2)
+            nc.vector.tensor_copy(picked[z][c][:, h, :], pairs[i][:].indirect(offsets_of(spans[z][c])))
+
+        def weave(z, c):
+            nc.scalar.copy(woven[z][:, 2 * spans[z][c].start : 2 * spans[z][c].stop].rearrange("p (j h) -> p j h", h=2), picked[z][c][:].rearrange("p h j -> p j h"))
+
+        def quantise(z, cols):
+            words = woven[z][:, 2 * cols.start : 2 * cols.stop]
+            nc.vector.quantize_mx(out=x_codes[z][:, cols].bitcast(FP8X4), scales=x_scales[z][:, cols], in_=words.bitcast(BF16))
+
+        def multiply(z, m, g):
+            cols = slice(P * g, P * (g + 1))
+            nc.tensor.matmul_mx(
+                out=acc[m][g][:],
+                lhsT=w_codes[:, z, 2 * P * m : 2 * P * (m + 1)].bitcast(FP4X4),
+                lhsT_scale=w_scales[:, z, P * m : P * (m + 1)],
+                rhs=x_codes[z][:, cols].bitcast(FP8X4),
+                rhs_scale=x_scales[z][:, cols],
+                start=(z == 0),
+                stop=(z == PASSES - 1),
+            )
+
+        def gate_side(m, cols, tag):
+            looked_up = keep.tile([P, cols.stop - cols.start], F32, name=tag, align_bytes=64)
+            nc.vector.tensor_copy(looked_up[:], side_rows[m][:].indirect(offsets_of(cols)))
+            nc.scalar.activation(gate[m][:, cols], looked_up[:], SILU)
+
+        def finish(m, c):
+            for g in (2 * c, 2 * c + 1):
+                cols = slice(P * g, P * (g + 1))
+                nc.vector.tensor_tensor(result[m][:, cols], acc[m][g][:], gate[m][:, cols], MULT)
+            cols = (first, second)[c]
+            nc.sync.dma_start(out=out[P * m : P * (m + 1), cols], in_=result[m][:, cols])
+
+        nc.vector.memset(w_scales[:].rearrange("p z c -> p (z c)").bitcast(I32), 0)
+        nc.sync.dma_start(offsets[:], offs)
+        load_side(0)
+        load_pair(0)
+        load_pair(1)
+        load_scales()
+        load_pair(2)
+        load_pair(3)
+        load_codes()
+        load_side(1)
+        gate_side(0, whole, "looked_up0")
+        cast_piece(0, 0)
+        gather_pair(0, 0)
+        cast_piece(1, 0)
+        gather_pair(1, 0)
+        cast_piece(2, 0)
+        weave(0, 0)
+        gather_pair(2, 0)
+        gather_pair(2, 1)
+        cast_piece(3, 0)
+        quantise(0, whole)
+        for g in range(4):
+            for m in range(2):
+                multiply(0, m, g)
+        gather_pair(3, 0)
+        gather_pair(3, 1)
+        weave(1, 0)
+        weave(1, 1)
+        gate_side(1, first, "raw3")
+        quantise(1, first)
+        gate_side(1, second, "picked1_0")
+        quantise(1, second)
+        for c in range(2):
+            for m in range(2):
+                for g in (2 * c, 2 * c + 1):
+                    multiply(1, m, g)
+        for c in range(2):
+            for m in range(2):
+                finish(m, c)

@@ -41,7 +41,7 @@ def tile_picked_sidegate_silu_l_kernel(tc, xT, side, w1_words, w1_scales, offs, 
         x_scales = [keep.tile([P, S], U8, name=f"x_scales{z}", align_bytes=64) for z in range(PASSES)]
         acc = [[psum.tile([P, P], F32, name=f"acc{m}_{g}") for g in range(4)] for m in range(2)]
 
-        pieces = [[[0,1024,672]],[[0,1024,672]],[[0,1024,640]],[[0,1024,352]]]
+        pieces = [[[0,1024,688]],[[0,1024,672]],[[0,1024,640]],[[0,1024,128]]]
         raw = [keep.tile([P, 2 * T + (2 * S - 16 if i == 2 else 0)], F32, name=f"raw{i}", align_bytes=64) for i in range(4)]
         woven = [raw[2][:, 2 * T - 16 :].bitcast(U32), keep.tile([P, 2 * S], U32, name="woven1", align_bytes=64)[:]]
 
@@ -57,7 +57,7 @@ def tile_picked_sidegate_silu_l_kernel(tc, xT, side, w1_words, w1_scales, offs, 
 
         def load_scales():
             for q in range(4):
-                nc.sync.dma_start(
+                nc.gpsimd.dma_start(
                     out=w_scales[32 * q : 32 * q + 4, :, :].bitcast(I32),
                     in_=w1_scales[:, 4 * q : 4 * q + 4, :].rearrange("z r c -> r z c").bitcast(I32),
                 )
@@ -105,24 +105,26 @@ def tile_picked_sidegate_silu_l_kernel(tc, xT, side, w1_words, w1_scales, offs, 
             nc.vector.tensor_copy(looked_up[:], side_rows[m][:].indirect(offsets_of(cols)))
             nc.scalar.activation(gate[m][:, cols], looked_up[:], SILU)
 
-        def finish(m, c):
-            for g in (2 * c, 2 * c + 1):
-                cols = slice(P * g, P * (g + 1))
-                nc.vector.tensor_tensor(result[m][:, cols], acc[m][g][:], gate[m][:, cols], MULT)
-            cols = (first, second)[c]
+        def apply_gate(m, g):
+            cols = slice(P * g, P * (g + 1))
+            nc.vector.tensor_tensor(result[m][:, cols], acc[m][g][:], gate[m][:, cols], MULT)
+
+        def store(m, cols):
             nc.sync.dma_start(out=out[P * m : P * (m + 1), cols], in_=result[m][:, cols])
 
-        nc.vector.memset(w_scales[:].rearrange("p z c -> p (z c)").bitcast(I32), 0)
+        nc.gpsimd.memset(w_scales[:].rearrange("p z c -> p (z c)").bitcast(I32), 0)
+        warm = keep.tile([P, 2], F32, name="warm")
+        nc.vector.memset(warm[:, 0:1], 0.0)
+        nc.scalar.activation(warm[:, 1:2], warm[:, 0:1], SILU)
+        load_scales()
         nc.sync.dma_start(offsets[:], offs)
-        load_side(0)
         load_pair(0)
         load_pair(1)
-        load_scales()
         load_pair(2)
         load_pair(3)
+        load_side(0)
         load_codes()
         load_side(1)
-        gate_side(0, whole, "looked_up0")
         cast_piece(0, 0)
         gather_pair(0, 0)
         cast_piece(1, 0)
@@ -131,8 +133,9 @@ def tile_picked_sidegate_silu_l_kernel(tc, xT, side, w1_words, w1_scales, offs, 
         weave(0, 0)
         gather_pair(2, 0)
         gather_pair(2, 1)
-        cast_piece(3, 0)
         quantise(0, whole)
+        cast_piece(3, 0)
+        gate_side(0, whole, "looked_up0")
         for g in range(4):
             for m in range(2):
                 multiply(0, m, g)
@@ -148,6 +151,7 @@ def tile_picked_sidegate_silu_l_kernel(tc, xT, side, w1_words, w1_scales, offs, 
             for m in range(2):
                 for g in (2 * c, 2 * c + 1):
                     multiply(1, m, g)
-        for c in range(2):
-            for m in range(2):
-                finish(m, c)
+        for m, cols in ((0, first), (1, first), (0, second), (1, slice(2 * P, 3 * P)), (1, slice(3 * P, 4 * P))):
+            for g in range(cols.start // P, cols.stop // P):
+                apply_gate(m, g)
+            store(m, cols)

@@ -57,7 +57,7 @@ def tile_picked_sidegate_silu_l_kernel(tc, xT, side, w1_words, w1_scales, offs, 
 
         def load_scales():
             for q in range(4):
-                nc.gpsimd.dma_start(
+                nc.sync.dma_start(
                     out=w_scales[32 * q : 32 * q + 4, :, :].bitcast(I32),
                     in_=w1_scales[:, 4 * q : 4 * q + 4, :].rearrange("z r c -> r z c").bitcast(I32),
                 )
@@ -112,11 +112,10 @@ def tile_picked_sidegate_silu_l_kernel(tc, xT, side, w1_words, w1_scales, offs, 
         def store(m, cols):
             nc.sync.dma_start(out=out[P * m : P * (m + 1), cols], in_=result[m][:, cols])
 
-        nc.gpsimd.memset(w_scales[:].rearrange("p z c -> p (z c)").bitcast(I32), 0)
+        nc.vector.memset(w_scales[:].rearrange("p z c -> p (z c)").bitcast(I32), 0)
         warm = keep.tile([P, 2], F32, name="warm")
         nc.vector.memset(warm[:, 0:1], 0.0)
         nc.scalar.activation(warm[:, 1:2], warm[:, 0:1], SILU)
-        load_scales()
         nc.sync.dma_start(offsets[:], offs)
         load_pair(0)
         load_pair(1)
@@ -125,6 +124,7 @@ def tile_picked_sidegate_silu_l_kernel(tc, xT, side, w1_words, w1_scales, offs, 
         load_side(0)
         load_codes()
         load_side(1)
+        load_scales()
         cast_piece(0, 0)
         gather_pair(0, 0)
         cast_piece(1, 0)

@@ -41,7 +41,7 @@ def tile_picked_sidegate_silu_l_kernel(tc, xT, side, w1_words, w1_scales, offs, 
         x_scales = [keep.tile([P, S], U8, name=f"x_scales{z}", align_bytes=64) for z in range(PASSES)]
         acc = [[psum.tile([P, P], F32, name=f"acc{m}_{g}") for g in range(4)] for m in range(2)]
 
-        pieces = [[[0,1024,688]],[[0,1024,672]],[[0,1024,640]],[[0,1024,128]]]
+        pieces = [[[0,1024,688]],[[0,1024,672]],[[0,1024,672]],[[0,1024,128]]]
         raw = [keep.tile([P, 2 * T + (2 * S - 16 if i == 2 else 0)], F32, name=f"raw{i}", align_bytes=64) for i in range(4)]
         woven = [raw[2][:, 2 * T - 16 :].bitcast(U32), keep.tile([P, 2 * S], U32, name="woven1", align_bytes=64)[:]]
 
@@ -122,8 +122,8 @@ def tile_picked_sidegate_silu_l_kernel(tc, xT, side, w1_words, w1_scales, offs, 
         load_pair(2)
         load_pair(3)
         load_side(0)
-        load_codes()
         load_side(1)
+        load_codes()
         load_scales()
         cast_piece(0, 0)
         gather_pair(0, 0)
@@ -143,15 +143,15 @@ def tile_picked_sidegate_silu_l_kernel(tc, xT, side, w1_words, w1_scales, offs, 
         gather_pair(3, 1)
         weave(1, 0)
         weave(1, 1)
-        gate_side(1, first, "raw3")
+        gate_side(1, slice(0, 320), "raw3")
         quantise(1, first)
-        gate_side(1, second, "picked1_0")
         quantise(1, second)
+        gate_side(1, slice(320, S), "picked1_1")
         for c in range(2):
             for m in range(2):
                 for g in (2 * c, 2 * c + 1):
                     multiply(1, m, g)
-        for m, cols in ((0, first), (1, first), (0, second), (1, slice(2 * P, 3 * P)), (1, slice(3 * P, 4 * P))):
+        for m, cols in ((0, first), (1, first), (0, second), (1, second)):
             for g in range(cols.start // P, cols.stop // P):
                 apply_gate(m, g)
             store(m, cols)

@@ -110,7 +110,8 @@ def tile_picked_sidegate_silu_l_kernel(tc, xT, side, w1_words, w1_scales, offs, 
             nc.vector.tensor_tensor(result[m][:, cols], acc[m][g][:], gate[m][:, cols], MULT)
 
         def store(m, cols):
-            nc.sync.dma_start(out=out[P * m : P * (m + 1), cols], in_=result[m][:, cols])
+            queue = nc.sync if m == 0 else nc.scalar
+            queue.dma_start(out=out[P * m : P * (m + 1), cols], in_=result[m][:, cols])
 
         nc.vector.memset(w_scales[:].rearrange("p z c -> p (z c)").bitcast(I32), 0)
         warm = keep.tile([P, 2], F32, name="warm")

@@ -13,12 +13,14 @@ U16 = mybir.dt.uint16
 U8 = mybir.dt.uint8
 FP8X4 = mybir.dt.float8_e4m3fn_x4
 FP4X4 = mybir.dt.float4_e2m1fn_x4
+COPY = mybir.ActivationFunctionType.Copy
 SILU = mybir.ActivationFunctionType.Silu
 MULT = mybir.AluOpType.mult
 
 P = 128
 PASSES = 2
 HALF = S // 2
+SHARE_SIDE = 384
 
 
 def tile_picked_sidegate_silu_l_kernel(tc, xT, side, w1_words, w1_scales, offs, out):
@@ -31,128 +33,110 @@ def tile_picked_sidegate_silu_l_kernel(tc, xT, side, w1_words, w1_scales, offs, 
         offsets = keep.tile([P, S // 16], U16, name="offsets")
         w_codes = keep.tile([P, PASSES, 2 * N], U8, name="w_codes", align_bytes=64)
         w_scales = keep.tile([P, PASSES, N], U8, name="w_scales", align_bytes=64)
-        side_rows = [keep.tile([P, T], F32, name=f"side_rows{m}") for m in range(2)]
-        gate = [keep.tile([P, S], F32, name=f"gate{m}") for m in range(2)]
-        result = [keep.tile([P, S], F32, name=f"result{m}") for m in range(2)]
-        pairs = [keep.tile([P, T], U32, name=f"pairs{i}") for i in range(4)]
-        spans = [[whole], [first, second]]
-        picked = [[keep.tile([P, 2, cols.stop - cols.start], U32, name=f"picked{z}_{c}", align_bytes=64) for c, cols in enumerate(spans[z])] for z in range(PASSES)]
+        raw = keep.tile([P, 8 * T], F32, name="raw")
+        place = [6, 7, 5, 4, 3, 2, 1, 0]
+        picked = [keep.tile([P, 2 * S], F32, name=f"picked{h}", align_bytes=64) for h in range(2)]
+        picked_456 = keep.tile([P, 3 * HALF], F32, name="picked_456", align_bytes=64)
+        picked_45 = keep.tile([P, 2 * HALF], F32, name="picked_45", align_bytes=64)
+        picked_67 = keep.tile([P, 2 * HALF], F32, name="picked_67", align_bytes=64)
+        woven0 = keep.tile([P, 4 * S], BF16, name="woven0", align_bytes=64)
+        woven1 = [keep.tile([P, 4 * HALF], BF16, name=f"woven1_{c}", align_bytes=64) for c in range(2)]
         x_codes = [keep.tile([P, S], U32, name=f"x_codes{z}", align_bytes=64) for z in range(PASSES)]
         x_scales = [keep.tile([P, S], U8, name=f"x_scales{z}", align_bytes=64) for z in range(PASSES)]
-        acc = [[psum.tile([P, P], F32, name=f"acc{m}_{g}") for g in range(4)] for m in range(2)]
+        side_rows = keep.tile([P, 2 * T], F32, name="side_rows")
+        looked_up0 = raw[:, 2 * T : 2 * T + S]
+        looked_up1 = picked_67[:]
+        looked_up1_rest = keep.tile([P, S], F32, name="looked_up1_rest", align_bytes=64)[:]
+        gate = [keep.tile([P, S], F32, name=f"gate{m}", align_bytes=64) for m in range(2)]
+        result = [keep.tile([P, S], F32, name=f"result{m}", align_bytes=64) for m in range(2)]
+        acc = [psum.tile([P, S], F32, name=f"acc{m}") for m in range(2)]
 
-        pieces = [[[0,1024,688]],[[0,1024,672]],[[0,1024,672]],[[0,1024,128]]]
-        raw = [keep.tile([P, 2 * T + (2 * S - 16 if i == 2 else 0)], F32, name=f"raw{i}", align_bytes=64) for i in range(4)]
-        woven = [raw[2][:, 2 * T - 16 :].bitcast(U32), keep.tile([P, 2 * S], U32, name="woven1", align_bytes=64)[:]]
+        def gather(on_vector, dst, window, cols):
+            source = window.indirect(offsets[:, cols.start // 16 : cols.stop // 16])
+            if on_vector:
+                nc.vector.tensor_copy(dst, source)
+            else:
+                nc.scalar.activation(dst, source, COPY)
 
+        def window(plane, planes):
+            return raw[:, T * place[plane] : T * min(place[plane] + planes, 8)]
 
-        def offsets_of(cols):
-            return offsets[:, cols.start // 16 : cols.stop // 16]
+        def slots(woven, first_slot, count):
+            return woven[:].rearrange("p (j t) -> p j t", t=4)[:, :, first_slot : first_slot + count]
 
-        def load_pair(i):
-            z, h = divmod(i, 2)
-            rows = xT[512 * z : 512 * (z + 1), :].rearrange("(p t) w -> p t w", t=4)
-            for n, (a, b, s) in enumerate(pieces[i]):
-                nc.sync.dma_start(out=raw[i][:, : 2 * T].rearrange("p (t w) -> p t w", t=2)[:, :, a:b], in_=rows[:, 2 * h : 2 * h + 2, a:b])
+        def weave(woven, first_slot, count, source):
+            nc.vector.tensor_copy(slots(woven, first_slot, count), source[:].rearrange("p (t j) -> p j t", t=count))
 
-        def load_scales():
-            for q in range(4):
-                nc.sync.dma_start(
-                    out=w_scales[32 * q : 32 * q + 4, :, :].bitcast(I32),
-                    in_=w1_scales[:, 4 * q : 4 * q + 4, :].rearrange("z r c -> r z c").bitcast(I32),
-                )
+        def quantise(z, cols, woven):
+            nc.vector.quantize_mx(out=x_codes[z][:, cols].bitcast(FP8X4), scales=x_scales[z][:, cols], in_=woven[:])
 
-        def load_side(m):
-            nc.sync.dma_start(out=side_rows[m][:], in_=side[P * m : P * (m + 1), :])
-
-        def load_codes():
-            nc.sync.dma_start(out=w_codes[:].bitcast(I32), in_=w1_words.rearrange("z p b -> p z b").bitcast(I32))
-
-        def cast_piece(i, n):
-            halves = pairs[i][:].bitcast(BF16).rearrange("p (w t) -> p w t", t=2)
-            a, b, s = pieces[i][n]
-            src = raw[i][:, : 2 * T].rearrange("p (t w) -> p w t", t=2)
-            if s < b:
-                nc.scalar.copy(halves[:, s:b, :], src[:, s:b, :])
-            if s > a:
-                nc.vector.tensor_copy(halves[:, a:s, :], src[:, a:s, :])
-
-        def gather_pair(i, c):
-            z, h = divmod(i, 2)
-            nc.vector.tensor_copy(picked[z][c][:, h, :], pairs[i][:].indirect(offsets_of(spans[z][c])))
-
-        def weave(z, c):
-            nc.scalar.copy(woven[z][:, 2 * spans[z][c].start : 2 * spans[z][c].stop].rearrange("p (j h) -> p j h", h=2), picked[z][c][:].rearrange("p h j -> p j h"))
-
-        def quantise(z, cols):
-            words = woven[z][:, 2 * cols.start : 2 * cols.stop]
-            nc.vector.quantize_mx(out=x_codes[z][:, cols].bitcast(FP8X4), scales=x_scales[z][:, cols], in_=words.bitcast(BF16))
-
-        def multiply(z, m, g):
-            cols = slice(P * g, P * (g + 1))
+        def multiply(z, m):
             nc.tensor.matmul_mx(
-                out=acc[m][g][:],
+                out=acc[m][:],
                 lhsT=w_codes[:, z, 2 * P * m : 2 * P * (m + 1)].bitcast(FP4X4),
                 lhsT_scale=w_scales[:, z, P * m : P * (m + 1)],
-                rhs=x_codes[z][:, cols].bitcast(FP8X4),
-                rhs_scale=x_scales[z][:, cols],
+                rhs=x_codes[z][:].bitcast(FP8X4),
+                rhs_scale=x_scales[z][:],
                 start=(z == 0),
                 stop=(z == PASSES - 1),
             )
 
-        def gate_side(m, cols, tag):
-            looked_up = keep.tile([P, cols.stop - cols.start], F32, name=tag, align_bytes=64)
-            nc.vector.tensor_copy(looked_up[:], side_rows[m][:].indirect(offsets_of(cols)))
-            nc.scalar.activation(gate[m][:, cols], looked_up[:], SILU)
+        def silu(m, source, cols):
+            nc.scalar.activation(gate[m][:, cols], source[:, cols], SILU)
 
-        def apply_gate(m, g):
-            cols = slice(P * g, P * (g + 1))
-            nc.vector.tensor_tensor(result[m][:, cols], acc[m][g][:], gate[m][:, cols], MULT)
-
-        def store(m, cols):
-            queue = nc.sync if m == 0 else nc.scalar
-            queue.dma_start(out=out[P * m : P * (m + 1), cols], in_=result[m][:, cols])
+        def finish(m, cols):
+            nc.vector.tensor_tensor(result[m][:, cols], acc[m][:, cols], gate[m][:, cols], MULT)
+            nc.sync.dma_start(out=out[P * m : P * (m + 1), cols], in_=result[m][:, cols])
 
         nc.vector.memset(w_scales[:].rearrange("p z c -> p (z c)").bitcast(I32), 0)
+        nc.sync.dma_start(offsets[:], offs)
+        for q in range(4):
+            nc.scalar.dma_start(
+                out=w_scales[32 * q : 32 * q + 4, :, :].bitcast(I32),
+                in_=w1_scales[:, 4 * q : 4 * q + 4, :].rearrange("z r c -> r z c").bitcast(I32),
+            )
+        nc.scalar.dma_start(out=w_codes[:].bitcast(I32), in_=w1_words.rearrange("z p b -> p z b").bitcast(I32))
         warm = keep.tile([P, 2], F32, name="warm")
         nc.vector.memset(warm[:, 0:1], 0.0)
         nc.scalar.activation(warm[:, 1:2], warm[:, 0:1], SILU)
-        nc.sync.dma_start(offsets[:], offs)
-        load_pair(0)
-        load_pair(1)
-        load_pair(2)
-        load_pair(3)
-        load_side(0)
-        load_side(1)
-        load_codes()
-        load_scales()
-        cast_piece(0, 0)
-        gather_pair(0, 0)
-        cast_piece(1, 0)
-        gather_pair(1, 0)
-        cast_piece(2, 0)
-        weave(0, 0)
-        gather_pair(2, 0)
-        gather_pair(2, 1)
-        quantise(0, whole)
-        cast_piece(3, 0)
-        gate_side(0, whole, "looked_up0")
-        for g in range(4):
-            for m in range(2):
-                multiply(0, m, g)
-        gather_pair(3, 0)
-        gather_pair(3, 1)
-        weave(1, 0)
-        weave(1, 1)
-        gate_side(1, slice(0, 320), "raw3")
-        quantise(1, first)
-        quantise(1, second)
-        gate_side(1, slice(320, S), "picked1_1")
-        for c in range(2):
-            for m in range(2):
-                for g in (2 * c, 2 * c + 1):
-                    multiply(1, m, g)
-        for m, cols in ((0, first), (1, first), (0, second), (1, second)):
-            for g in range(cols.start // P, cols.stop // P):
-                apply_gate(m, g)
-            store(m, cols)
+        for plane, count in [(0, 2), (2, 1), (3, 1), (4, 1), (5, 1), (6, 1), (7, 1)]:
+            z, t = divmod(plane, 4)
+            rows = xT[512 * z : 512 * (z + 1), :].rearrange("(p t) w -> p (t w)", t=4)
+            nc.sync.dma_start(out=window(plane, count), in_=rows[:, T * t : T * (t + count)])
+        for m in range(2):
+            nc.sync.dma_start(out=side_rows[:, T * (1 - m) : T * (2 - m)], in_=side[P * m : P * (m + 1), :])
+
+        gather(True, picked[0][:, :S], window(0, 1), whole)
+        gather(False, picked[0][:, S:], window(1, 1), whole)
+        gather(False, picked[1][:, :S], window(2, 4), whole)
+        weave(woven0, 0, 2, picked[0])
+        gather(True, picked[1][:, S : S + HALF], window(3, 2), first)
+        gather(False, picked[1][:, S + HALF :], window(3, 4), second)
+        gather(False, picked_456[:, :HALF], window(4, 4), first)
+        gather(False, picked_45[:, :HALF], window(4, 4), second)
+        weave(woven0, 2, 2, picked[1])
+        gather(True, picked_456[:, HALF : 2 * HALF], window(5, 2), first)
+        gather(False, picked_45[:, HALF:], window(5, 4), second)
+        quantise(0, whole, woven0)
+        for m in range(2):
+            multiply(0, m)
+        gather(False, picked_456[:, 2 * HALF :], window(6, 4), first)
+        gather(False, picked_67[:, :HALF], window(6, 4), second)
+        weave(woven1[1], 0, 2, picked_45)
+        weave(woven1[0], 0, 3, picked_456)
+        gather(True, woven1[0][:, 3 :: 4], window(7, 1), first)
+        gather(False, picked_67[:, HALF:], window(7, 2), second)
+        weave(woven1[1], 2, 2, picked_67)
+        quantise(1, first, woven1[0])
+        quantise(1, second, woven1[1])
+        for m in range(2):
+            multiply(1, m)
+        gather(False, looked_up0, side_rows[:, T:], whole)
+        gather(True, looked_up1[:, :SHARE_SIDE], side_rows[:, :T], slice(0, SHARE_SIDE))
+        gather(False, looked_up1_rest[:, SHARE_SIDE:], side_rows[:], slice(SHARE_SIDE, S))
+        silu(0, looked_up0, whole)
+        silu(1, looked_up1, slice(0, SHARE_SIDE))
+        silu(1, looked_up1_rest, slice(SHARE_SIDE, S))
+        finish(0, whole)
+        finish(1, slice(0, SHARE_SIDE))
+        finish(1, slice(SHARE_SIDE, S))

@@ -31,7 +31,7 @@ def tile_picked_sidegate_silu_l_kernel(tc, xT, side, w1_words, w1_scales, offs, 
 
         first, second, whole = slice(0, HALF), slice(HALF, S), slice(0, S)
         offsets = keep.tile([P, S // 16], U16, name="offsets")
-        w_codes = keep.tile([P, PASSES, 2 * N], U8, name="w_codes", align_bytes=64)
+        w_codes = [keep.tile([P, 2 * N], U8, name=f"w_codes{z}", align_bytes=64) for z in range(PASSES)]
         w_scales = keep.tile([P, PASSES, N], U8, name="w_scales", align_bytes=64)
         raw = keep.tile([P, 8 * T], F32, name="raw")
         place = [6, 7, 5, 4, 3, 2, 1, 0]
@@ -73,7 +73,7 @@ def tile_picked_sidegate_silu_l_kernel(tc, xT, side, w1_words, w1_scales, offs, 
         def multiply(z, m):
             nc.tensor.matmul_mx(
                 out=acc[m][:],
-                lhsT=w_codes[:, z, 2 * P * m : 2 * P * (m + 1)].bitcast(FP4X4),
+                lhsT=w_codes[z][:, 2 * P * m : 2 * P * (m + 1)].bitcast(FP4X4),
                 lhsT_scale=w_scales[:, z, P * m : P * (m + 1)],
                 rhs=x_codes[z][:].bitcast(FP8X4),
                 rhs_scale=x_scales[z][:],
@@ -88,14 +88,13 @@ def tile_picked_sidegate_silu_l_kernel(tc, xT, side, w1_words, w1_scales, offs, 
             nc.vector.tensor_tensor(result[m][:, cols], acc[m][:, cols], gate[m][:, cols], MULT)
             nc.sync.dma_start(out=out[P * m : P * (m + 1), cols], in_=result[m][:, cols])
 
-        nc.vector.memset(w_scales[:].rearrange("p z c -> p (z c)").bitcast(I32), 0)
+        nc.gpsimd.memset(w_scales[:].rearrange("p z c -> p (z c)").bitcast(I32), 0)
         nc.sync.dma_start(offsets[:], offs)
         for q in range(4):
-            nc.scalar.dma_start(
+            nc.gpsimd.dma_start(
                 out=w_scales[32 * q : 32 * q + 4, :, :].bitcast(I32),
                 in_=w1_scales[:, 4 * q : 4 * q + 4, :].rearrange("z r c -> r z c").bitcast(I32),
             )
-        nc.scalar.dma_start(out=w_codes[:].bitcast(I32), in_=w1_words.rearrange("z p b -> p z b").bitcast(I32))
         warm = keep.tile([P, 2], F32, name="warm")
         nc.vector.memset(warm[:, 0:1], 0.0)
         nc.scalar.activation(warm[:, 1:2], warm[:, 0:1], SILU)
@@ -105,6 +104,7 @@ def tile_picked_sidegate_silu_l_kernel(tc, xT, side, w1_words, w1_scales, offs, 
             nc.sync.dma_start(out=window(plane, count), in_=rows[:, T * t : T * (t + count)])
         for m in range(2):
             nc.sync.dma_start(out=side_rows[:, T * (1 - m) : T * (2 - m)], in_=side[P * m : P * (m + 1), :])
+            nc.sync.dma_start(out=w_codes[m][:].bitcast(I32), in_=w1_words[m].bitcast(I32))
 
         gather(True, picked[0][:, :S], window(0, 1), whole)
         gather(False, picked[0][:, S:], window(1, 1), whole)

@@ -20,7 +20,7 @@ MULT = mybir.AluOpType.mult
 P = 128
 PASSES = 2
 HALF = S // 2
-SHARE_SIDE = 384
+PIECE = 160
 
 
 def tile_picked_sidegate_silu_l_kernel(tc, xT, side, w1_words, w1_scales, offs, out):
@@ -30,11 +30,12 @@ def tile_picked_sidegate_silu_l_kernel(tc, xT, side, w1_words, w1_scales, offs, 
         psum = ctx.enter_context(tc.psum_pool(name="psum", bufs=1))
 
         first, second, whole = slice(0, HALF), slice(HALF, S), slice(0, S)
+        halves = (first, second)
         offsets = keep.tile([P, S // 16], U16, name="offsets")
         w_codes = [keep.tile([P, 2 * N], U8, name=f"w_codes{z}", align_bytes=64) for z in range(PASSES)]
         w_scales = keep.tile([P, PASSES, N], U8, name="w_scales", align_bytes=64)
         raw = keep.tile([P, 8 * T], F32, name="raw")
-        place = [6, 7, 5, 4, 3, 2, 1, 0]
+        place = [6, 7, 4, 5, 3, 2, 1, 0]
         picked = [keep.tile([P, 2 * S], F32, name=f"picked{h}", align_bytes=64) for h in range(2)]
         picked_456 = keep.tile([P, 3 * HALF], F32, name="picked_456", align_bytes=64)
         picked_45 = keep.tile([P, 2 * HALF], F32, name="picked_45", align_bytes=64)
@@ -49,7 +50,7 @@ def tile_picked_sidegate_silu_l_kernel(tc, xT, side, w1_words, w1_scales, offs, 
         looked_up1_rest = keep.tile([P, S], F32, name="looked_up1_rest", align_bytes=64)[:]
         gate = [keep.tile([P, S], F32, name=f"gate{m}", align_bytes=64) for m in range(2)]
         result = [keep.tile([P, S], F32, name=f"result{m}", align_bytes=64) for m in range(2)]
-        acc = [psum.tile([P, S], F32, name=f"acc{m}") for m in range(2)]
+        acc = [[psum.tile([P, HALF], F32, name=f"acc{m}_{c}") for c in range(2)] for m in range(2)]
 
         def gather(on_vector, dst, window, cols):
             source = window.indirect(offsets[:, cols.start // 16 : cols.stop // 16])
@@ -70,13 +71,14 @@ def tile_picked_sidegate_silu_l_kernel(tc, xT, side, w1_words, w1_scales, offs, 
         def quantise(z, cols, woven):
             nc.vector.quantize_mx(out=x_codes[z][:, cols].bitcast(FP8X4), scales=x_scales[z][:, cols], in_=woven[:])
 
-        def multiply(z, m):
+        def multiply(z, m, c):
+            cols = halves[c]
             nc.tensor.matmul_mx(
-                out=acc[m][:],
+                out=acc[m][c][:],
                 lhsT=w_codes[z][:, 2 * P * m : 2 * P * (m + 1)].bitcast(FP4X4),
                 lhsT_scale=w_scales[:, z, P * m : P * (m + 1)],
-                rhs=x_codes[z][:].bitcast(FP8X4),
-                rhs_scale=x_scales[z][:],
+                rhs=x_codes[z][:, cols].bitcast(FP8X4),
+                rhs_scale=x_scales[z][:, cols],
                 start=(z == 0),
                 stop=(z == PASSES - 1),
             )
@@ -84,21 +86,24 @@ def tile_picked_sidegate_silu_l_kernel(tc, xT, side, w1_words, w1_scales, offs, 
         def silu(m, source, cols):
             nc.scalar.activation(gate[m][:, cols], source[:, cols], SILU)
 
-        def finish(m, cols):
-            nc.vector.tensor_tensor(result[m][:, cols], acc[m][:, cols], gate[m][:, cols], MULT)
+        def apply_gate(m, c):
+            cols = halves[c]
+            nc.vector.tensor_tensor(result[m][:, cols], acc[m][c][:], gate[m][:, cols], MULT)
+
+        def store(m, cols):
             nc.sync.dma_start(out=out[P * m : P * (m + 1), cols], in_=result[m][:, cols])
 
         nc.gpsimd.memset(w_scales[:].rearrange("p z c -> p (z c)").bitcast(I32), 0)
         nc.sync.dma_start(offsets[:], offs)
         for q in range(4):
-            nc.gpsimd.dma_start(
+            nc.scalar.dma_start(
                 out=w_scales[32 * q : 32 * q + 4, :, :].bitcast(I32),
                 in_=w1_scales[:, 4 * q : 4 * q + 4, :].rearrange("z r c -> r z c").bitcast(I32),
             )
         warm = keep.tile([P, 2], F32, name="warm")
         nc.vector.memset(warm[:, 0:1], 0.0)
         nc.scalar.activation(warm[:, 1:2], warm[:, 0:1], SILU)
-        for plane, count in [(0, 2), (2, 1), (3, 1), (4, 1), (5, 1), (6, 1), (7, 1)]:
+        for plane, count in [(0, 2), (2, 2), (4, 1), (5, 1), (6, 1), (7, 1)]:
             z, t = divmod(plane, 4)
             rows = xT[512 * z : 512 * (z + 1), :].rearrange("(p t) w -> p (t w)", t=4)
             nc.sync.dma_start(out=window(plane, count), in_=rows[:, T * t : T * (t + count)])
@@ -108,18 +113,19 @@ def tile_picked_sidegate_silu_l_kernel(tc, xT, side, w1_words, w1_scales, offs, 
 
         gather(True, picked[0][:, :S], window(0, 1), whole)
         gather(False, picked[0][:, S:], window(1, 1), whole)
-        gather(False, picked[1][:, :S], window(2, 4), whole)
         weave(woven0, 0, 2, picked[0])
-        gather(True, picked[1][:, S : S + HALF], window(3, 2), first)
-        gather(False, picked[1][:, S + HALF :], window(3, 4), second)
+        gather(True, picked[1][:, :S], window(2, 4), whole)
+        gather(False, picked[1][:, S:], window(3, 4), whole)
         gather(False, picked_456[:, :HALF], window(4, 4), first)
         gather(False, picked_45[:, :HALF], window(4, 4), second)
         weave(woven0, 2, 2, picked[1])
-        gather(True, picked_456[:, HALF : 2 * HALF], window(5, 2), first)
+        gather(True, picked_456[:, HALF : HALF + 192], window(5, 1), slice(0, 192))
+        gather(False, picked_456[:, HALF + 192 : 2 * HALF], window(5, 4), slice(192, HALF))
         gather(False, picked_45[:, HALF:], window(5, 4), second)
         quantise(0, whole, woven0)
         for m in range(2):
-            multiply(0, m)
+            for c in range(2):
+                multiply(0, m, c)
         gather(False, picked_456[:, 2 * HALF :], window(6, 4), first)
         gather(False, picked_67[:, :HALF], window(6, 4), second)
         weave(woven1[1], 0, 2, picked_45)
@@ -130,13 +136,22 @@ def tile_picked_sidegate_silu_l_kernel(tc, xT, side, w1_words, w1_scales, offs, 
         quantise(1, first, woven1[0])
         quantise(1, second, woven1[1])
         for m in range(2):
-            multiply(1, m)
-        gather(False, looked_up0, side_rows[:, T:], whole)
-        gather(True, looked_up1[:, :SHARE_SIDE], side_rows[:, :T], slice(0, SHARE_SIDE))
-        gather(False, looked_up1_rest[:, SHARE_SIDE:], side_rows[:], slice(SHARE_SIDE, S))
-        silu(0, looked_up0, whole)
-        silu(1, looked_up1, slice(0, SHARE_SIDE))
-        silu(1, looked_up1_rest, slice(SHARE_SIDE, S))
-        finish(0, whole)
-        finish(1, slice(0, SHARE_SIDE))
-        finish(1, slice(SHARE_SIDE, S))
+            for c in range(2):
+                multiply(1, m, c)
+        for cols in (first, second):
+            gather(False, looked_up0[:, cols], side_rows[:, T:], cols)
+        pieces = [slice(0, PIECE), slice(PIECE, 2 * PIECE), slice(2 * PIECE, S)]
+        for cols in pieces[:2]:
+            gather(True, looked_up1[:, cols], side_rows[:, :T], cols)
+        for cols in (first, second):
+            silu(0, looked_up0, cols)
+        gather(False, looked_up1_rest[:, pieces[2]], side_rows[:], pieces[2])
+        for cols in pieces[:2]:
+            silu(1, looked_up1, cols)
+        silu(1, looked_up1_rest, pieces[2])
+        for c in range(2):
+            apply_gate(0, c)
+        store(0, whole)
+        for c in range(2):
+            apply_gate(1, c)
+            store(1, halves[c])

@@ -20,7 +20,7 @@ MULT = mybir.AluOpType.mult
 P = 128
 PASSES = 2
 HALF = S // 2
-PIECE = 160
+SHARE_SIDE = (192, 128)
 
 
 def tile_picked_sidegate_silu_l_kernel(tc, xT, side, w1_words, w1_scales, offs, out):
@@ -47,7 +47,6 @@ def tile_picked_sidegate_silu_l_kernel(tc, xT, side, w1_words, w1_scales, offs, 
         side_rows = keep.tile([P, 2 * T], F32, name="side_rows")
         looked_up0 = raw[:, 2 * T : 2 * T + S]
         looked_up1 = picked_67[:]
-        looked_up1_rest = keep.tile([P, S], F32, name="looked_up1_rest", align_bytes=64)[:]
         gate = [keep.tile([P, S], F32, name=f"gate{m}", align_bytes=64) for m in range(2)]
         result = [keep.tile([P, S], F32, name=f"result{m}", align_bytes=64) for m in range(2)]
         acc = [[psum.tile([P, HALF], F32, name=f"acc{m}_{c}") for c in range(2)] for m in range(2)]
@@ -140,18 +139,17 @@ def tile_picked_sidegate_silu_l_kernel(tc, xT, side, w1_words, w1_scales, offs, 
                 multiply(1, m, c)
         for cols in (first, second):
             gather(False, looked_up0[:, cols], side_rows[:, T:], cols)
-        pieces = [slice(0, PIECE), slice(PIECE, 2 * PIECE), slice(2 * PIECE, S)]
-        for cols in pieces[:2]:
-            gather(True, looked_up1[:, cols], side_rows[:, :T], cols)
-        for cols in (first, second):
+        for cols, share in zip(halves, SHARE_SIDE):
+            piece = slice(cols.start, cols.start + share)
+            gather(True, looked_up1[:, piece], side_rows[:, :T], piece)
+        for cols in halves:
             silu(0, looked_up0, cols)
-        gather(False, looked_up1_rest[:, pieces[2]], side_rows[:], pieces[2])
-        for cols in pieces[:2]:
+        for cols, share in zip(halves, SHARE_SIDE):
+            piece = slice(cols.start + share, cols.stop)
+            gather(False, looked_up1[:, piece], side_rows[:], piece)
+        for cols in halves:
             silu(1, looked_up1, cols)
-        silu(1, looked_up1_rest, pieces[2])
-        for c in range(2):
-            apply_gate(0, c)
-        store(0, whole)
-        for c in range(2):
-            apply_gate(1, c)
-            store(1, halves[c])
+        for m in range(2):
+            for c in range(2):
+                apply_gate(m, c)
+            store(m, whole)

@@ -152,4 +152,4 @@ def tile_picked_sidegate_silu_l_kernel(tc, xT, side, w1_words, w1_scales, offs, 
         for m in range(2):
             for c in range(2):
                 apply_gate(m, c)
-            store(m, whole)
+                store(m, halves[c])

@@ -92,13 +92,8 @@ def tile_picked_sidegate_silu_l_kernel(tc, xT, side, w1_words, w1_scales, offs, 
         def store(m, cols):
             nc.sync.dma_start(out=out[P * m : P * (m + 1), cols], in_=result[m][:, cols])
 
-        nc.gpsimd.memset(w_scales[:].rearrange("p z c -> p (z c)").bitcast(I32), 0)
+        nc.vector.memset(w_scales[:].rearrange("p z c -> p (z c)").bitcast(I32), 0)
         nc.sync.dma_start(offsets[:], offs)
-        for q in range(4):
-            nc.scalar.dma_start(
-                out=w_scales[32 * q : 32 * q + 4, :, :].bitcast(I32),
-                in_=w1_scales[:, 4 * q : 4 * q + 4, :].rearrange("z r c -> r z c").bitcast(I32),
-            )
         warm = keep.tile([P, 2], F32, name="warm")
         nc.vector.memset(warm[:, 0:1], 0.0)
         nc.scalar.activation(warm[:, 1:2], warm[:, 0:1], SILU)
@@ -106,6 +101,12 @@ def tile_picked_sidegate_silu_l_kernel(tc, xT, side, w1_words, w1_scales, offs, 
             z, t = divmod(plane, 4)
             rows = xT[512 * z : 512 * (z + 1), :].rearrange("(p t) w -> p (t w)", t=4)
             nc.sync.dma_start(out=window(plane, count), in_=rows[:, T * t : T * (t + count)])
+            if plane == 0:
+                for q in range(4):
+                    nc.sync.dma_start(
+                        out=w_scales[32 * q : 32 * q + 4, :, :].bitcast(I32),
+                        in_=w1_scales[:, 4 * q : 4 * q + 4, :].rearrange("z r c -> r z c").bitcast(I32),
+                    )
         for m in range(2):
             nc.sync.dma_start(out=side_rows[:, T * (1 - m) : T * (2 - m)], in_=side[P * m : P * (m + 1), :])
             nc.sync.dma_start(out=w_codes[m][:].bitcast(I32), in_=w1_words[m].bitcast(I32))

@@ -18,9 +18,14 @@ SILU = mybir.ActivationFunctionType.Silu
 MULT = mybir.AluOpType.mult
 
 P = 128
-PASSES = 2
+SLOTS = 4
+K_PASS = P * SLOTS
+PASSES = K // K_PASS
+ROW_TILES = N // P
 HALF = S // 2
-SHARE_SIDE = (192, 128)
+X_LOADS = ((0, 2), (2, 2), (4, 1), (5, 1), (6, 1), (7, 1))
+VECTOR_SHARE_PLANE_5 = 192
+VECTOR_SHARE_SIDE_1 = (192, 128)
 
 
 def tile_picked_sidegate_silu_l_kernel(tc, xT, side, w1_words, w1_scales, offs, out):
@@ -34,123 +39,114 @@ def tile_picked_sidegate_silu_l_kernel(tc, xT, side, w1_words, w1_scales, offs, 
         offsets = keep.tile([P, S // 16], U16, name="offsets")
         w_codes = [keep.tile([P, 2 * N], U8, name=f"w_codes{z}", align_bytes=64) for z in range(PASSES)]
         w_scales = keep.tile([P, PASSES, N], U8, name="w_scales", align_bytes=64)
-        raw = keep.tile([P, 8 * T], F32, name="raw")
-        place = [6, 7, 4, 5, 3, 2, 1, 0]
-        picked = [keep.tile([P, 2 * S], F32, name=f"picked{h}", align_bytes=64) for h in range(2)]
+        x_rows = keep.tile([P, PASSES * SLOTS * T], F32, name="x_rows")
+        planes = [x_rows[:, T * plane : T * (plane + 1)] for plane in range(PASSES * SLOTS)]
+        picked_01 = keep.tile([P, 2 * S], F32, name="picked_01", align_bytes=64)
+        picked_23 = keep.tile([P, 2 * S], F32, name="picked_23", align_bytes=64)
         picked_456 = keep.tile([P, 3 * HALF], F32, name="picked_456", align_bytes=64)
         picked_45 = keep.tile([P, 2 * HALF], F32, name="picked_45", align_bytes=64)
         picked_67 = keep.tile([P, 2 * HALF], F32, name="picked_67", align_bytes=64)
-        woven0 = keep.tile([P, 4 * S], BF16, name="woven0", align_bytes=64)
-        woven1 = [keep.tile([P, 4 * HALF], BF16, name=f"woven1_{c}", align_bytes=64) for c in range(2)]
+        woven0 = keep.tile([P, SLOTS * S], BF16, name="woven0", align_bytes=64)
+        woven1 = [keep.tile([P, SLOTS * HALF], BF16, name=f"woven1_{c}", align_bytes=64) for c in range(2)]
         x_codes = [keep.tile([P, S], U32, name=f"x_codes{z}", align_bytes=64) for z in range(PASSES)]
         x_scales = [keep.tile([P, S], U8, name=f"x_scales{z}", align_bytes=64) for z in range(PASSES)]
-        side_rows = keep.tile([P, 2 * T], F32, name="side_rows")
-        looked_up0 = raw[:, 2 * T : 2 * T + S]
-        looked_up1 = picked_67[:]
-        gate = [keep.tile([P, S], F32, name=f"gate{m}", align_bytes=64) for m in range(2)]
-        result = [keep.tile([P, S], F32, name=f"result{m}", align_bytes=64) for m in range(2)]
-        acc = [[psum.tile([P, HALF], F32, name=f"acc{m}_{c}") for c in range(2)] for m in range(2)]
+        side_rows = [keep.tile([P, T], F32, name=f"side_rows{m}") for m in range(ROW_TILES)]
+        side_picked = [planes[6][:, :S], picked_67[:]]
+        gate = [keep.tile([P, S], F32, name=f"gate{m}", align_bytes=64) for m in range(ROW_TILES)]
+        result = [keep.tile([P, S], F32, name=f"result{m}", align_bytes=64) for m in range(ROW_TILES)]
+        acc = [[psum.tile([P, HALF], F32, name=f"acc{m}_{c}") for c in range(2)] for m in range(ROW_TILES)]
 
-        def gather(on_vector, dst, window, cols):
-            source = window.indirect(offsets[:, cols.start // 16 : cols.stop // 16])
-            if on_vector:
-                nc.vector.tensor_copy(dst, source)
-            else:
-                nc.scalar.activation(dst, source, COPY)
+        def listed(window, entries):
+            return window.indirect(offsets[:, entries.start // 16 : entries.stop // 16])
 
-        def window(plane, planes):
-            return raw[:, T * place[plane] : T * min(place[plane] + planes, 8)]
+        def vector_gather(dst, window, entries):
+            nc.vector.tensor_copy(dst, listed(window, entries))
 
-        def slots(woven, first_slot, count):
-            return woven[:].rearrange("p (j t) -> p j t", t=4)[:, :, first_slot : first_slot + count]
+        def scalar_gather(dst, window, entries):
+            nc.scalar.activation(dst, listed(window, entries), COPY)
 
-        def weave(woven, first_slot, count, source):
-            nc.vector.tensor_copy(slots(woven, first_slot, count), source[:].rearrange("p (t j) -> p j t", t=count))
+        def weave(woven, first_slot, count, picked):
+            slots = woven[:].rearrange("p (j t) -> p j t", t=SLOTS)[:, :, first_slot : first_slot + count]
+            nc.vector.tensor_copy(slots, picked[:].rearrange("p (t j) -> p j t", t=count))
 
-        def quantise(z, cols, woven):
-            nc.vector.quantize_mx(out=x_codes[z][:, cols].bitcast(FP8X4), scales=x_scales[z][:, cols], in_=woven[:])
+        def quantise(z, entries, woven):
+            nc.vector.quantize_mx(out=x_codes[z][:, entries].bitcast(FP8X4), scales=x_scales[z][:, entries], in_=woven[:])
 
-        def multiply(z, m, c):
-            cols = halves[c]
-            nc.tensor.matmul_mx(
-                out=acc[m][c][:],
-                lhsT=w_codes[z][:, 2 * P * m : 2 * P * (m + 1)].bitcast(FP4X4),
-                lhsT_scale=w_scales[:, z, P * m : P * (m + 1)],
-                rhs=x_codes[z][:, cols].bitcast(FP8X4),
-                rhs_scale=x_scales[z][:, cols],
-                start=(z == 0),
-                stop=(z == PASSES - 1),
-            )
+        def multiply(z):
+            for m in range(ROW_TILES):
+                for c, entries in enumerate(halves):
+                    nc.tensor.matmul_mx(
+                        out=acc[m][c][:],
+                        lhsT=w_codes[z][:, 2 * P * m : 2 * P * (m + 1)].bitcast(FP4X4),
+                        lhsT_scale=w_scales[:, z, P * m : P * (m + 1)],
+                        rhs=x_codes[z][:, entries].bitcast(FP8X4),
+                        rhs_scale=x_scales[z][:, entries],
+                        start=(z == 0),
+                        stop=(z == PASSES - 1),
+                    )
 
-        def silu(m, source, cols):
-            nc.scalar.activation(gate[m][:, cols], source[:, cols], SILU)
-
-        def apply_gate(m, c):
-            cols = halves[c]
-            nc.vector.tensor_tensor(result[m][:, cols], acc[m][c][:], gate[m][:, cols], MULT)
-
-        def store(m, cols):
-            nc.sync.dma_start(out=out[P * m : P * (m + 1), cols], in_=result[m][:, cols])
+        def silu(m):
+            for entries in halves:
+                nc.scalar.activation(gate[m][:, entries], side_picked[m][:, entries], SILU)
 
         nc.vector.memset(w_scales[:].rearrange("p z c -> p (z c)").bitcast(I32), 0)
         nc.sync.dma_start(offsets[:], offs)
         warm = keep.tile([P, 2], F32, name="warm")
         nc.vector.memset(warm[:, 0:1], 0.0)
         nc.scalar.activation(warm[:, 1:2], warm[:, 0:1], SILU)
-        for plane, count in [(0, 2), (2, 2), (4, 1), (5, 1), (6, 1), (7, 1)]:
-            z, t = divmod(plane, 4)
-            rows = xT[512 * z : 512 * (z + 1), :].rearrange("(p t) w -> p (t w)", t=4)
-            nc.sync.dma_start(out=window(plane, count), in_=rows[:, T * t : T * (t + count)])
+
+        for plane, count in X_LOADS:
+            z, t = divmod(plane, SLOTS)
+            rows = xT[K_PASS * z : K_PASS * (z + 1), :].rearrange("(p t) w -> p (t w)", t=SLOTS)
+            nc.sync.dma_start(out=x_rows[:, T * plane : T * (plane + count)], in_=rows[:, T * t : T * (t + count)])
             if plane == 0:
                 for q in range(4):
                     nc.sync.dma_start(
                         out=w_scales[32 * q : 32 * q + 4, :, :].bitcast(I32),
                         in_=w1_scales[:, 4 * q : 4 * q + 4, :].rearrange("z r c -> r z c").bitcast(I32),
                     )
-        for m in range(2):
-            nc.sync.dma_start(out=side_rows[:, T * (1 - m) : T * (2 - m)], in_=side[P * m : P * (m + 1), :])
-            nc.sync.dma_start(out=w_codes[m][:].bitcast(I32), in_=w1_words[m].bitcast(I32))
+        for i in range(2):
+            nc.sync.dma_start(out=side_rows[i][:], in_=side[P * i : P * (i + 1), :])
+            nc.sync.dma_start(out=w_codes[i][:].bitcast(I32), in_=w1_words[i].bitcast(I32))
 
-        gather(True, picked[0][:, :S], window(0, 1), whole)
-        gather(False, picked[0][:, S:], window(1, 1), whole)
-        weave(woven0, 0, 2, picked[0])
-        gather(True, picked[1][:, :S], window(2, 4), whole)
-        gather(False, picked[1][:, S:], window(3, 4), whole)
-        gather(False, picked_456[:, :HALF], window(4, 4), first)
-        gather(False, picked_45[:, :HALF], window(4, 4), second)
-        weave(woven0, 2, 2, picked[1])
-        gather(True, picked_456[:, HALF : HALF + 192], window(5, 1), slice(0, 192))
-        gather(False, picked_456[:, HALF + 192 : 2 * HALF], window(5, 4), slice(192, HALF))
-        gather(False, picked_45[:, HALF:], window(5, 4), second)
+        vector_gather(picked_01[:, :S], planes[0], whole)
+        scalar_gather(picked_01[:, S:], planes[1], whole)
+        weave(woven0, 0, 2, picked_01)
+        vector_gather(picked_23[:, :S], planes[2], whole)
+        scalar_gather(picked_23[:, S:], planes[3], whole)
+        scalar_gather(picked_456[:, :HALF], planes[4], first)
+        scalar_gather(picked_45[:, :HALF], planes[4], second)
+        weave(woven0, 2, 2, picked_23)
+        cut = VECTOR_SHARE_PLANE_5
+        vector_gather(picked_456[:, HALF : HALF + cut], planes[5], slice(0, cut))
+        scalar_gather(picked_456[:, HALF + cut : 2 * HALF], planes[5], slice(cut, HALF))
+        scalar_gather(picked_45[:, HALF:], planes[5], second)
         quantise(0, whole, woven0)
-        for m in range(2):
-            for c in range(2):
-                multiply(0, m, c)
-        gather(False, picked_456[:, 2 * HALF :], window(6, 4), first)
-        gather(False, picked_67[:, :HALF], window(6, 4), second)
+        multiply(0)
+
+        scalar_gather(picked_456[:, 2 * HALF :], planes[6], first)
+        scalar_gather(picked_67[:, :HALF], planes[6], second)
         weave(woven1[1], 0, 2, picked_45)
         weave(woven1[0], 0, 3, picked_456)
-        gather(True, woven1[0][:, 3 :: 4], window(7, 1), first)
-        gather(False, picked_67[:, HALF:], window(7, 2), second)
+        vector_gather(woven1[0][:, SLOTS - 1 :: SLOTS], planes[7], first)
+        scalar_gather(picked_67[:, HALF:], planes[7], second)
         weave(woven1[1], 2, 2, picked_67)
-        quantise(1, first, woven1[0])
-        quantise(1, second, woven1[1])
-        for m in range(2):
-            for c in range(2):
-                multiply(1, m, c)
-        for cols in (first, second):
-            gather(False, looked_up0[:, cols], side_rows[:, T:], cols)
-        for cols, share in zip(halves, SHARE_SIDE):
-            piece = slice(cols.start, cols.start + share)
-            gather(True, looked_up1[:, piece], side_rows[:, :T], piece)
-        for cols in halves:
-            silu(0, looked_up0, cols)
-        for cols, share in zip(halves, SHARE_SIDE):
-            piece = slice(cols.start + share, cols.stop)
-            gather(False, looked_up1[:, piece], side_rows[:], piece)
-        for cols in halves:
-            silu(1, looked_up1, cols)
-        for m in range(2):
-            for c in range(2):
-                apply_gate(m, c)
-                store(m, halves[c])
+        for entries, woven in zip(halves, woven1):
+            quantise(1, entries, woven)
+        multiply(1)
+
+        for entries in halves:
+            scalar_gather(side_picked[0][:, entries], side_rows[0][:], entries)
+        for entries, share in zip(halves, VECTOR_SHARE_SIDE_1):
+            head = slice(entries.start, entries.start + share)
+            vector_gather(side_picked[1][:, head], side_rows[1][:], head)
+        silu(0)
+        for entries, share in zip(halves, VECTOR_SHARE_SIDE_1):
+            tail = slice(entries.start + share, entries.stop)
+            scalar_gather(side_picked[1][:, tail], side_rows[1][:], tail)
+        silu(1)
+
+        for m in range(ROW_TILES):
+            for c, entries in enumerate(halves):
+                nc.vector.tensor_tensor(result[m][:, entries], acc[m][c][:], gate[m][:, entries], MULT)
+                nc.sync.dma_start(out=out[P * m : P * (m + 1), entries], in_=result[m][:, entries])

@@ -23,9 +23,10 @@ K_PASS = P * SLOTS
 PASSES = K // K_PASS
 ROW_TILES = N // P
 HALF = S // 2
-X_LOADS = ((0, 2), (2, 2), (4, 1), (5, 1), (6, 1), (7, 1))
+X_LOADS = ((0, 2), (2, 1), (3, 1), (4, 1), (5, 1), (6, 1), (7, 1))
 VECTOR_SHARE_PLANE_5 = 192
-VECTOR_SHARE_SIDE_1 = (192, 128)
+VECTOR_SHARE_SIDE_1 = 128
+QUARTER = S // 4
 
 
 def tile_picked_sidegate_silu_l_kernel(tc, xT, side, w1_words, w1_scales, offs, out):
@@ -43,15 +44,14 @@ def tile_picked_sidegate_silu_l_kernel(tc, xT, side, w1_words, w1_scales, offs, 
         planes = [x_rows[:, T * plane : T * (plane + 1)] for plane in range(PASSES * SLOTS)]
         picked_01 = keep.tile([P, 2 * S], F32, name="picked_01", align_bytes=64)
         picked_23 = keep.tile([P, 2 * S], F32, name="picked_23", align_bytes=64)
-        picked_456 = keep.tile([P, 3 * HALF], F32, name="picked_456", align_bytes=64)
-        picked_45 = keep.tile([P, 2 * HALF], F32, name="picked_45", align_bytes=64)
-        picked_67 = keep.tile([P, 2 * HALF], F32, name="picked_67", align_bytes=64)
+        picked_45 = [keep.tile([P, 2 * HALF], F32, name=f"picked_45_{c}", align_bytes=64) for c in range(2)]
+        picked_67 = [keep.tile([P, 2 * HALF], F32, name=f"picked_67_{c}", align_bytes=64) for c in range(2)]
         woven0 = keep.tile([P, SLOTS * S], BF16, name="woven0", align_bytes=64)
         woven1 = [keep.tile([P, SLOTS * HALF], BF16, name=f"woven1_{c}", align_bytes=64) for c in range(2)]
         x_codes = [keep.tile([P, S], U32, name=f"x_codes{z}", align_bytes=64) for z in range(PASSES)]
         x_scales = [keep.tile([P, S], U8, name=f"x_scales{z}", align_bytes=64) for z in range(PASSES)]
         side_rows = [keep.tile([P, T], F32, name=f"side_rows{m}") for m in range(ROW_TILES)]
-        side_picked = [planes[6][:, :S], picked_67[:]]
+        side_picked = [planes[6][:, :S], picked_67[1][:]]
         gate = [keep.tile([P, S], F32, name=f"gate{m}", align_bytes=64) for m in range(ROW_TILES)]
         result = [keep.tile([P, S], F32, name=f"result{m}", align_bytes=64) for m in range(ROW_TILES)]
         acc = [[psum.tile([P, HALF], F32, name=f"acc{m}_{c}") for c in range(2)] for m in range(ROW_TILES)]
@@ -65,12 +65,12 @@ def tile_picked_sidegate_silu_l_kernel(tc, xT, side, w1_words, w1_scales, offs, 
         def scalar_gather(dst, window, entries):
             nc.scalar.activation(dst, listed(window, entries), COPY)
 
-        def weave(woven, first_slot, count, picked):
-            slots = woven[:].rearrange("p (j t) -> p j t", t=SLOTS)[:, :, first_slot : first_slot + count]
-            nc.vector.tensor_copy(slots, picked[:].rearrange("p (t j) -> p j t", t=count))
+        def weave(woven, first_slot, count, picked, entries=slice(None)):
+            slots = woven[:].rearrange("p (j t) -> p j t", t=SLOTS)[:, entries, first_slot : first_slot + count]
+            nc.vector.tensor_copy(slots, picked[:].rearrange("p (t j) -> p j t", t=count)[:, entries, :])
 
         def quantise(z, entries, woven):
-            nc.vector.quantize_mx(out=x_codes[z][:, entries].bitcast(FP8X4), scales=x_scales[z][:, entries], in_=woven[:])
+            nc.vector.quantize_mx(out=x_codes[z][:, entries].bitcast(FP8X4), scales=x_scales[z][:, entries], in_=woven)
 
         def multiply(z):
             for m in range(ROW_TILES):
@@ -90,7 +90,6 @@ def tile_picked_sidegate_silu_l_kernel(tc, xT, side, w1_words, w1_scales, offs, 
                 nc.scalar.activation(gate[m][:, entries], side_picked[m][:, entries], SILU)
 
         nc.vector.memset(w_scales[:].rearrange("p z c -> p (z c)").bitcast(I32), 0)
-        nc.sync.dma_start(offsets[:], offs)
         warm = keep.tile([P, 2], F32, name="warm")
         nc.vector.memset(warm[:, 0:1], 0.0)
         nc.scalar.activation(warm[:, 1:2], warm[:, 0:1], SILU)
@@ -100,6 +99,7 @@ def tile_picked_sidegate_silu_l_kernel(tc, xT, side, w1_words, w1_scales, offs, 
             rows = xT[K_PASS * z : K_PASS * (z + 1), :].rearrange("(p t) w -> p (t w)", t=SLOTS)
             nc.sync.dma_start(out=x_rows[:, T * plane : T * (plane + count)], in_=rows[:, T * t : T * (t + count)])
             if plane == 0:
+                nc.sync.dma_start(offsets[:], offs)
                 for q in range(4):
                     nc.sync.dma_start(
                         out=w_scales[32 * q : 32 * q + 4, :, :].bitcast(I32),
@@ -109,41 +109,46 @@ def tile_picked_sidegate_silu_l_kernel(tc, xT, side, w1_words, w1_scales, offs, 
             nc.sync.dma_start(out=side_rows[i][:], in_=side[P * i : P * (i + 1), :])
             nc.sync.dma_start(out=w_codes[i][:].bitcast(I32), in_=w1_words[i].bitcast(I32))
 
+        quarters = [slice(QUARTER * i, QUARTER * (i + 1)) for i in range(4)]
         vector_gather(picked_01[:, :S], planes[0], whole)
         scalar_gather(picked_01[:, S:], planes[1], whole)
         weave(woven0, 0, 2, picked_01)
-        vector_gather(picked_23[:, :S], planes[2], whole)
-        scalar_gather(picked_23[:, S:], planes[3], whole)
-        scalar_gather(picked_456[:, :HALF], planes[4], first)
-        scalar_gather(picked_45[:, :HALF], planes[4], second)
-        weave(woven0, 2, 2, picked_23)
-        cut = VECTOR_SHARE_PLANE_5
-        vector_gather(picked_456[:, HALF : HALF + cut], planes[5], slice(0, cut))
-        scalar_gather(picked_456[:, HALF + cut : 2 * HALF], planes[5], slice(cut, HALF))
-        scalar_gather(picked_45[:, HALF:], planes[5], second)
-        quantise(0, whole, woven0)
+        scalar_gather(picked_23[:, :S], planes[2], whole)
+        vector_gather(picked_23[:, S : S + HALF], planes[3], first)
+        scalar_gather(picked_23[:, S + HALF :], planes[3], second)
+        for entries in halves:
+            weave(woven0, 2, 2, picked_23, entries)
+        for entries in halves:
+            quantise(0, entries, woven0[:, SLOTS * entries.start : SLOTS * entries.stop])
         multiply(0)
 
-        scalar_gather(picked_456[:, 2 * HALF :], planes[6], first)
-        scalar_gather(picked_67[:, :HALF], planes[6], second)
-        weave(woven1[1], 0, 2, picked_45)
-        weave(woven1[0], 0, 3, picked_456)
-        vector_gather(woven1[0][:, SLOTS - 1 :: SLOTS], planes[7], first)
-        scalar_gather(picked_67[:, HALF:], planes[7], second)
-        weave(woven1[1], 2, 2, picked_67)
+        for c, entries in enumerate(halves):
+            scalar_gather(picked_45[c][:, :HALF], planes[4], entries)
+        cut = S - VECTOR_SHARE_PLANE_5
+        scalar_gather(picked_45[0][:, HALF:], planes[5], first)
+        scalar_gather(picked_45[1][:, HALF:cut], planes[5], slice(HALF, cut))
+        vector_gather(picked_45[1][:, cut:], planes[5], slice(cut, S))
+        for c in range(2):
+            weave(woven1[c], 0, 2, picked_45[c])
+        scalar_gather(picked_67[0][:, :HALF], planes[6], first)
+        scalar_gather(picked_67[1][:, :QUARTER], planes[6], quarters[2])
+        vector_gather(picked_67[1][:, QUARTER:HALF], planes[6], quarters[3])
+        for c in range(2):
+            vector_gather(picked_67[c][:, HALF : HALF + QUARTER], planes[7], quarters[2 * c])
+            scalar_gather(picked_67[c][:, HALF + QUARTER :], planes[7], quarters[2 * c + 1])
+        for c in range(2):
+            weave(woven1[c], 2, 2, picked_67[c])
         for entries, woven in zip(halves, woven1):
-            quantise(1, entries, woven)
+            quantise(1, entries, woven[:])
         multiply(1)
 
         for entries in halves:
             scalar_gather(side_picked[0][:, entries], side_rows[0][:], entries)
-        for entries, share in zip(halves, VECTOR_SHARE_SIDE_1):
-            head = slice(entries.start, entries.start + share)
-            vector_gather(side_picked[1][:, head], side_rows[1][:], head)
+        cut = HALF + VECTOR_SHARE_SIDE_1
+        vector_gather(side_picked[1][:, first], side_rows[1][:], first)
+        vector_gather(side_picked[1][:, HALF:cut], side_rows[1][:], slice(HALF, cut))
         silu(0)
-        for entries, share in zip(halves, VECTOR_SHARE_SIDE_1):
-            tail = slice(entries.start + share, entries.stop)
-            scalar_gather(side_picked[1][:, tail], side_rows[1][:], tail)
+        scalar_gather(side_picked[1][:, cut:], side_rows[1][:], slice(cut, S))
         silu(1)
 
         for m in range(ROW_TILES):

@@ -23,10 +23,13 @@ K_PASS = P * SLOTS
 PASSES = K // K_PASS
 ROW_TILES = N // P
 HALF = S // 2
-X_LOADS = ((0, 2), (2, 1), (3, 1), (4, 1), (5, 1), (6, 1), (7, 1))
-VECTOR_SHARE_PLANE_5 = 192
-VECTOR_SHARE_SIDE_1 = 128
 QUARTER = S // 4
+X_LOADS = ((0, 2), (2, 2), (4, 2), (6, 1), (7, 1))
+SCALAR_SHARE_SIDE_1 = 128
+SCALAR_WEAVES = 64
+VECTOR_SHARE_PLANE_5 = 256
+VECTOR_SHARE_PLANE_6 = 352
+RUN = 4
 
 
 def tile_picked_sidegate_silu_l_kernel(tc, xT, side, w1_words, w1_scales, offs, out):
@@ -35,23 +38,20 @@ def tile_picked_sidegate_silu_l_kernel(tc, xT, side, w1_words, w1_scales, offs, 
         keep = ctx.enter_context(tc.tile_pool(name="keep", bufs=1))
         psum = ctx.enter_context(tc.psum_pool(name="psum", bufs=1))
 
-        first, second, whole = slice(0, HALF), slice(HALF, S), slice(0, S)
-        halves = (first, second)
+        halves = [slice(HALF * c, HALF * (c + 1)) for c in range(2)]
+        quarters = [slice(QUARTER * i, QUARTER * (i + 1)) for i in range(4)]
         offsets = keep.tile([P, S // 16], U16, name="offsets")
         w_codes = [keep.tile([P, 2 * N], U8, name=f"w_codes{z}", align_bytes=64) for z in range(PASSES)]
         w_scales = keep.tile([P, PASSES, N], U8, name="w_scales", align_bytes=64)
-        x_rows = keep.tile([P, PASSES * SLOTS * T], F32, name="x_rows")
-        planes = [x_rows[:, T * plane : T * (plane + 1)] for plane in range(PASSES * SLOTS)]
-        picked_01 = keep.tile([P, 2 * S], F32, name="picked_01", align_bytes=64)
-        picked_23 = keep.tile([P, 2 * S], F32, name="picked_23", align_bytes=64)
-        picked_45 = [keep.tile([P, 2 * HALF], F32, name=f"picked_45_{c}", align_bytes=64) for c in range(2)]
-        picked_67 = [keep.tile([P, 2 * HALF], F32, name=f"picked_67_{c}", align_bytes=64) for c in range(2)]
-        woven0 = keep.tile([P, SLOTS * S], BF16, name="woven0", align_bytes=64)
-        woven1 = [keep.tile([P, SLOTS * HALF], BF16, name=f"woven1_{c}", align_bytes=64) for c in range(2)]
+        x_rows = [keep.tile([P, count * T], F32, name=f"x_rows{plane}") for plane, count in X_LOADS]
+        planes = [rows[:, T * i : T * (i + 1)] for rows, load in zip(x_rows, X_LOADS) for i in range(load[1])]
+        picked0 = [keep.tile([P, SLOTS * HALF], F32, name=f"picked0_{c}", align_bytes=64) for c in range(2)]
+        picked1 = keep.tile([P, SLOTS * S], F32, name="picked1", align_bytes=64)
+        woven = [[keep.tile([P, SLOTS * HALF], BF16, name=f"woven{z}_{c}", align_bytes=64) for c in range(2)] for z in range(PASSES)]
         x_codes = [keep.tile([P, S], U32, name=f"x_codes{z}", align_bytes=64) for z in range(PASSES)]
         x_scales = [keep.tile([P, S], U8, name=f"x_scales{z}", align_bytes=64) for z in range(PASSES)]
         side_rows = [keep.tile([P, T], F32, name=f"side_rows{m}") for m in range(ROW_TILES)]
-        side_picked = [planes[6][:, :S], picked_67[1][:]]
+        side_picked = [keep.tile([P, S], F32, name=f"side_picked{m}", align_bytes=64) for m in range(ROW_TILES)]
         gate = [keep.tile([P, S], F32, name=f"gate{m}", align_bytes=64) for m in range(ROW_TILES)]
         result = [keep.tile([P, S], F32, name=f"result{m}", align_bytes=64) for m in range(ROW_TILES)]
         acc = [[psum.tile([P, HALF], F32, name=f"acc{m}_{c}") for c in range(2)] for m in range(ROW_TILES)]
@@ -59,45 +59,69 @@ def tile_picked_sidegate_silu_l_kernel(tc, xT, side, w1_words, w1_scales, offs, 
         def listed(window, entries):
             return window.indirect(offsets[:, entries.start // 16 : entries.stop // 16])
 
-        def vector_gather(dst, window, entries):
-            nc.vector.tensor_copy(dst, listed(window, entries))
+        def gather(engine, dst, window, entries):
+            if engine == "vector":
+                nc.vector.tensor_copy(dst, listed(window, entries))
+            else:
+                nc.scalar.activation(dst, listed(window, entries), COPY)
 
-        def scalar_gather(dst, window, entries):
-            nc.scalar.activation(dst, listed(window, entries), COPY)
+        def gather_plane(engine, plane, entries):
+            z, t = divmod(plane, SLOTS)
+            if z == 0:
+                dst = picked0[entries.start // HALF][:, HALF * t : HALF * (t + 1)]
+            else:
+                dst = picked1[:, S * t + entries.start : S * t + entries.stop]
+            gather(engine, dst, planes[plane], entries)
 
-        def weave(woven, first_slot, count, picked, entries=slice(None)):
-            slots = woven[:].rearrange("p (j t) -> p j t", t=SLOTS)[:, entries, first_slot : first_slot + count]
-            nc.vector.tensor_copy(slots, picked[:].rearrange("p (t j) -> p j t", t=count)[:, entries, :])
+        def gather_side(engine, m, entries):
+            gather(engine, side_picked[m][:, entries], side_rows[m][:], entries)
 
-        def quantise(z, entries, woven):
-            nc.vector.quantize_mx(out=x_codes[z][:, entries].bitcast(FP8X4), scales=x_scales[z][:, entries], in_=woven)
+        def weave_four(copy, entries):
+            c, start = divmod(entries.start, HALF)
+            count = entries.stop - entries.start
+            copy(
+                woven[1][c][:, SLOTS * start : SLOTS * (start + count)].rearrange("p (g i t) -> p g t i", i=RUN, t=SLOTS),
+                picked1[:].rearrange("p (t g i) -> p g t i", i=RUN, t=SLOTS)[:, entries.start // RUN : entries.stop // RUN],
+            )
 
-        def multiply(z):
-            for m in range(ROW_TILES):
-                for c, entries in enumerate(halves):
-                    nc.tensor.matmul_mx(
-                        out=acc[m][c][:],
-                        lhsT=w_codes[z][:, 2 * P * m : 2 * P * (m + 1)].bitcast(FP4X4),
-                        lhsT_scale=w_scales[:, z, P * m : P * (m + 1)],
-                        rhs=x_codes[z][:, entries].bitcast(FP8X4),
-                        rhs_scale=x_scales[z][:, entries],
-                        start=(z == 0),
-                        stop=(z == PASSES - 1),
-                    )
+        def weave_pair(c, first):
+            slots = woven[0][c][:].rearrange("p (j t) -> p j t", t=SLOTS)[:, :, first : first + 2]
+            pair = picked0[c][:, HALF * first : HALF * (first + 2)]
+            nc.vector.tensor_copy(slots, pair.rearrange("p (t j) -> p j t", t=2))
 
-        def silu(m):
-            for entries in halves:
-                nc.scalar.activation(gate[m][:, entries], side_picked[m][:, entries], SILU)
+        def quantise(z, c):
+            nc.vector.quantize_mx(
+                out=x_codes[z][:, halves[c]].bitcast(FP8X4), scales=x_scales[z][:, halves[c]], in_=woven[z][c][:]
+            )
+
+        def multiply(z, m):
+            for c in range(2):
+                nc.tensor.matmul_mx(
+                    out=acc[m][c][:],
+                    lhsT=w_codes[z][:, 2 * P * m : 2 * P * (m + 1)].bitcast(FP4X4),
+                    lhsT_scale=w_scales[:, z, P * m : P * (m + 1)],
+                    rhs=x_codes[z][:, halves[c]].bitcast(FP8X4),
+                    rhs_scale=x_scales[z][:, halves[c]],
+                    start=(z == 0),
+                    stop=(z == PASSES - 1),
+                )
+
+        def silu(m, c):
+            nc.scalar.activation(gate[m][:, halves[c]], side_picked[m][:, halves[c]], SILU)
+
+        def finish(m, c):
+            nc.vector.tensor_tensor(result[m][:, halves[c]], acc[m][c][:], gate[m][:, halves[c]], MULT)
+            nc.sync.dma_start(out=out[P * m : P * (m + 1), halves[c]], in_=result[m][:, halves[c]])
 
         nc.vector.memset(w_scales[:].rearrange("p z c -> p (z c)").bitcast(I32), 0)
         warm = keep.tile([P, 2], F32, name="warm")
         nc.vector.memset(warm[:, 0:1], 0.0)
         nc.scalar.activation(warm[:, 1:2], warm[:, 0:1], SILU)
 
-        for plane, count in X_LOADS:
+        for (plane, count), loaded in zip(X_LOADS, x_rows):
             z, t = divmod(plane, SLOTS)
             rows = xT[K_PASS * z : K_PASS * (z + 1), :].rearrange("(p t) w -> p (t w)", t=SLOTS)
-            nc.sync.dma_start(out=x_rows[:, T * plane : T * (plane + count)], in_=rows[:, T * t : T * (t + count)])
+            nc.sync.dma_start(out=loaded[:], in_=rows[:, T * t : T * (t + count)])
             if plane == 0:
                 nc.sync.dma_start(offsets[:], offs)
                 for q in range(4):
@@ -109,49 +133,42 @@ def tile_picked_sidegate_silu_l_kernel(tc, xT, side, w1_words, w1_scales, offs, 
             nc.sync.dma_start(out=side_rows[i][:], in_=side[P * i : P * (i + 1), :])
             nc.sync.dma_start(out=w_codes[i][:].bitcast(I32), in_=w1_words[i].bitcast(I32))
 
-        quarters = [slice(QUARTER * i, QUARTER * (i + 1)) for i in range(4)]
-        vector_gather(picked_01[:, :S], planes[0], whole)
-        scalar_gather(picked_01[:, S:], planes[1], whole)
-        weave(woven0, 0, 2, picked_01)
-        scalar_gather(picked_23[:, :S], planes[2], whole)
-        vector_gather(picked_23[:, S : S + HALF], planes[3], first)
-        scalar_gather(picked_23[:, S + HALF :], planes[3], second)
-        for entries in halves:
-            weave(woven0, 2, 2, picked_23, entries)
-        for entries in halves:
-            quantise(0, entries, woven0[:, SLOTS * entries.start : SLOTS * entries.stop])
-        multiply(0)
-
-        for c, entries in enumerate(halves):
-            scalar_gather(picked_45[c][:, :HALF], planes[4], entries)
-        cut = S - VECTOR_SHARE_PLANE_5
-        scalar_gather(picked_45[0][:, HALF:], planes[5], first)
-        scalar_gather(picked_45[1][:, HALF:cut], planes[5], slice(HALF, cut))
-        vector_gather(picked_45[1][:, cut:], planes[5], slice(cut, S))
+        for pair in (0, 2):
+            for entries in halves:
+                gather_plane("vector", pair, entries)
+                gather_plane("scalar", pair + 1, entries)
+            for c in range(2):
+                weave_pair(c, pair)
         for c in range(2):
-            weave(woven1[c], 0, 2, picked_45[c])
-        scalar_gather(picked_67[0][:, :HALF], planes[6], first)
-        scalar_gather(picked_67[1][:, :QUARTER], planes[6], quarters[2])
-        vector_gather(picked_67[1][:, QUARTER:HALF], planes[6], quarters[3])
-        for c in range(2):
-            vector_gather(picked_67[c][:, HALF : HALF + QUARTER], planes[7], quarters[2 * c])
-            scalar_gather(picked_67[c][:, HALF + QUARTER :], planes[7], quarters[2 * c + 1])
-        for c in range(2):
-            weave(woven1[c], 2, 2, picked_67[c])
-        for entries, woven in zip(halves, woven1):
-            quantise(1, entries, woven[:])
-        multiply(1)
-
-        for entries in halves:
-            scalar_gather(side_picked[0][:, entries], side_rows[0][:], entries)
-        cut = HALF + VECTOR_SHARE_SIDE_1
-        vector_gather(side_picked[1][:, first], side_rows[1][:], first)
-        vector_gather(side_picked[1][:, HALF:cut], side_rows[1][:], slice(HALF, cut))
-        silu(0)
-        scalar_gather(side_picked[1][:, cut:], side_rows[1][:], slice(cut, S))
-        silu(1)
-
+            quantise(0, c)
         for m in range(ROW_TILES):
-            for c, entries in enumerate(halves):
-                nc.vector.tensor_tensor(result[m][:, entries], acc[m][c][:], gate[m][:, entries], MULT)
-                nc.sync.dma_start(out=out[P * m : P * (m + 1), entries], in_=result[m][:, entries])
+            multiply(0, m)
+
+        gather_plane("scalar", 4, slice(0, S))
+        for plane, share in ((5, VECTOR_SHARE_PLANE_5), (6, VECTOR_SHARE_PLANE_6)):
+            gather_plane("vector", plane, slice(0, share))
+            gather_plane("scalar", plane, slice(share, S))
+        for c in range(2):
+            gather_plane("vector", 7, quarters[2 * c])
+            gather_plane("scalar", 7, quarters[2 * c + 1])
+        weave_four(nc.vector.tensor_copy, slice(0, HALF - SCALAR_WEAVES))
+        weave_four(nc.scalar.copy, slice(HALF - SCALAR_WEAVES, HALF))
+        weave_four(nc.vector.tensor_copy, halves[1])
+        for c in range(2):
+            quantise(1, c)
+        for m in range(ROW_TILES):
+            multiply(1, m)
+
+        for entries in halves:
+            gather_side("scalar", 0, entries)
+        cut = S - SCALAR_SHARE_SIDE_1
+        gather_side("vector", 1, halves[0])
+        gather_side("vector", 1, slice(HALF, cut))
+        for c in range(2):
+            silu(0, c)
+        gather_side("scalar", 1, slice(cut, S))
+        for c in range(2):
+            silu(1, c)
+        for m in range(ROW_TILES):
+            for c in range(2):
+                finish(m, c)

@@ -41,19 +41,19 @@ def tile_picked_sidegate_silu_l_kernel(tc, xT, side, w1_words, w1_scales, offs, 
         halves = [slice(HALF * c, HALF * (c + 1)) for c in range(2)]
         quarters = [slice(QUARTER * i, QUARTER * (i + 1)) for i in range(4)]
         offsets = keep.tile([P, S // 16], U16, name="offsets")
-        w_codes = [keep.tile([P, 2 * N], U8, name=f"w_codes{z}", align_bytes=64) for z in range(PASSES)]
-        w_scales = keep.tile([P, PASSES, N], U8, name="w_scales", align_bytes=64)
-        x_rows = [keep.tile([P, count * T], F32, name=f"x_rows{plane}") for plane, count in X_LOADS]
+        w_codes = [keep.tile([P, 2 * N], U8, name=f"w_codes{z}", align_bytes=256) for z in range(PASSES)]
+        w_scales = keep.tile([P, PASSES, N], U8, name="w_scales", align_bytes=256)
+        x_rows = [keep.tile([P, count * T], F32, name=f"x_rows{plane}", align_bytes=256) for plane, count in X_LOADS]
         planes = [rows[:, T * i : T * (i + 1)] for rows, load in zip(x_rows, X_LOADS) for i in range(load[1])]
         picked0 = [keep.tile([P, SLOTS * HALF], F32, name=f"picked0_{c}", align_bytes=64) for c in range(2)]
         picked1 = keep.tile([P, SLOTS * S], F32, name="picked1", align_bytes=64)
         woven = [[keep.tile([P, SLOTS * HALF], BF16, name=f"woven{z}_{c}", align_bytes=64) for c in range(2)] for z in range(PASSES)]
         x_codes = [keep.tile([P, S], U32, name=f"x_codes{z}", align_bytes=64) for z in range(PASSES)]
         x_scales = [keep.tile([P, S], U8, name=f"x_scales{z}", align_bytes=64) for z in range(PASSES)]
-        side_rows = [keep.tile([P, T], F32, name=f"side_rows{m}") for m in range(ROW_TILES)]
+        side_rows = [keep.tile([P, T], F32, name=f"side_rows{m}", align_bytes=256) for m in range(ROW_TILES)]
         side_picked = [keep.tile([P, S], F32, name=f"side_picked{m}", align_bytes=64) for m in range(ROW_TILES)]
         gate = [keep.tile([P, S], F32, name=f"gate{m}", align_bytes=64) for m in range(ROW_TILES)]
-        result = [keep.tile([P, S], F32, name=f"result{m}", align_bytes=64) for m in range(ROW_TILES)]
+        result = [keep.tile([P, S], F32, name=f"result{m}", align_bytes=256) for m in range(ROW_TILES)]
         acc = [[psum.tile([P, HALF], F32, name=f"acc{m}_{c}") for c in range(2)] for m in range(ROW_TILES)]
 
         def listed(window, entries):

@@ -42,7 +42,7 @@ def tile_picked_sidegate_silu_l_kernel(tc, xT, side, w1_words, w1_scales, offs, 
         quarters = [slice(QUARTER * i, QUARTER * (i + 1)) for i in range(4)]
         offsets = keep.tile([P, S // 16], U16, name="offsets")
         w_codes = [keep.tile([P, 2 * N], U8, name=f"w_codes{z}", align_bytes=256) for z in range(PASSES)]
-        w_scales = keep.tile([P, PASSES, N], U8, name="w_scales", align_bytes=256)
+        w_scales = keep.tile([P, PASSES, 2, N], U8, name="w_scales", align_bytes=256)
         x_rows = [keep.tile([P, count * T], F32, name=f"x_rows{plane}", align_bytes=256) for plane, count in X_LOADS]
         planes = [rows[:, T * i : T * (i + 1)] for rows, load in zip(x_rows, X_LOADS) for i in range(load[1])]
         picked0 = [keep.tile([P, SLOTS * HALF], F32, name=f"picked0_{c}", align_bytes=64) for c in range(2)]
@@ -84,10 +84,10 @@ def tile_picked_sidegate_silu_l_kernel(tc, xT, side, w1_words, w1_scales, offs, 
                 picked1[:].rearrange("p (t g i) -> p g t i", i=RUN, t=SLOTS)[:, entries.start // RUN : entries.stop // RUN],
             )
 
-        def weave_pair(c, first):
+        def weave_pair(copy, c, first):
             slots = woven[0][c][:].rearrange("p (j t) -> p j t", t=SLOTS)[:, :, first : first + 2]
             pair = picked0[c][:, HALF * first : HALF * (first + 2)]
-            nc.vector.tensor_copy(slots, pair.rearrange("p (t j) -> p j t", t=2))
+            copy(slots, pair.rearrange("p (t j) -> p j t", t=2))
 
         def quantise(z, c):
             nc.vector.quantize_mx(
@@ -99,7 +99,7 @@ def tile_picked_sidegate_silu_l_kernel(tc, xT, side, w1_words, w1_scales, offs, 
                 nc.tensor.matmul_mx(
                     out=acc[m][c][:],
                     lhsT=w_codes[z][:, 2 * P * m : 2 * P * (m + 1)].bitcast(FP4X4),
-                    lhsT_scale=w_scales[:, z, P * m : P * (m + 1)],
+                    lhsT_scale=w_scales[:, z, 0, P * m : P * (m + 1)],
                     rhs=x_codes[z][:, halves[c]].bitcast(FP8X4),
                     rhs_scale=x_scales[z][:, halves[c]],
                     start=(z == 0),
@@ -113,7 +113,7 @@ def tile_picked_sidegate_silu_l_kernel(tc, xT, side, w1_words, w1_scales, offs, 
             nc.vector.tensor_tensor(result[m][:, halves[c]], acc[m][c][:], gate[m][:, halves[c]], MULT)
             nc.sync.dma_start(out=out[P * m : P * (m + 1), halves[c]], in_=result[m][:, halves[c]])
 
-        nc.vector.memset(w_scales[:].rearrange("p z c -> p (z c)").bitcast(I32), 0)
+        nc.vector.memset(w_scales[:].rearrange("p z h c -> p (z h c)").bitcast(I32), 0)
         warm = keep.tile([P, 2], F32, name="warm")
         nc.vector.memset(warm[:, 0:1], 0.0)
         nc.scalar.activation(warm[:, 1:2], warm[:, 0:1], SILU)
@@ -124,10 +124,10 @@ def tile_picked_sidegate_silu_l_kernel(tc, xT, side, w1_words, w1_scales, offs, 
             nc.sync.dma_start(out=loaded[:], in_=rows[:, T * t : T * (t + count)])
             if plane == 0:
                 nc.sync.dma_start(offsets[:], offs)
-                for q in range(4):
+                for q in range(2):
                     nc.sync.dma_start(
-                        out=w_scales[32 * q : 32 * q + 4, :, :].bitcast(I32),
-                        in_=w1_scales[:, 4 * q : 4 * q + 4, :].rearrange("z r c -> r z c").bitcast(I32),
+                        out=w_scales[32 * q : 32 * q + 4].rearrange("r z h c -> r (z h) c").bitcast(I32),
+                        in_=w1_scales.rearrange("z (h q r) c -> q r (z h) c", h=2, q=2)[q].bitcast(I32),
                     )
         for i in range(2):
             nc.sync.dma_start(out=side_rows[i][:], in_=side[P * i : P * (i + 1), :])
@@ -137,8 +137,11 @@ def tile_picked_sidegate_silu_l_kernel(tc, xT, side, w1_words, w1_scales, offs, 
             for entries in halves:
                 gather_plane("vector", pair, entries)
                 gather_plane("scalar", pair + 1, entries)
-            for c in range(2):
-                weave_pair(c, pair)
+            weave_pair(nc.vector.tensor_copy, 0, pair)
+            weave_pair(nc.scalar.copy if pair == 0 else nc.vector.tensor_copy, 1, pair)
+            if pair == 0:
+                for z in range(PASSES):
+                    nc.vector.tensor_copy(w_scales[64:128, z, 0, :].bitcast(I32), w_scales[0:64, z, 1, :].bitcast(I32))
         for c in range(2):
             quantise(0, c)
         for m in range(ROW_TILES):

@@ -68,7 +68,8 @@ def tile_picked_sidegate_silu_l_kernel(tc, xT, side, w1_words, w1_scales, offs, 
         def gather_plane(engine, plane, entries):
             z, t = divmod(plane, SLOTS)
             if z == 0:
-                dst = picked0[entries.start // HALF][:, HALF * t : HALF * (t + 1)]
+                c, start = divmod(entries.start, HALF)
+                dst = picked0[c][:, HALF * t + start : HALF * t + start + entries.stop - entries.start]
             else:
                 dst = picked1[:, S * t + entries.start : S * t + entries.stop]
             gather(engine, dst, planes[plane], entries)
@@ -76,12 +77,13 @@ def tile_picked_sidegate_silu_l_kernel(tc, xT, side, w1_words, w1_scales, offs, 
         def gather_side(engine, m, entries):
             gather(engine, side_picked[m][:, entries], side_rows[m][:], entries)
 
-        def weave_four(copy, entries):
+        def weave_four(copy, z, entries):
             c, start = divmod(entries.start, HALF)
             count = entries.stop - entries.start
+            source, first = (picked1, entries.start) if z == 1 else (picked0[c], start)
             copy(
-                woven[1][c][:, SLOTS * start : SLOTS * (start + count)].rearrange("p (g i t) -> p g t i", i=RUN, t=SLOTS),
-                picked1[:].rearrange("p (t g i) -> p g t i", i=RUN, t=SLOTS)[:, entries.start // RUN : entries.stop // RUN],
+                woven[z][c][:, SLOTS * start : SLOTS * (start + count)].rearrange("p (g i t) -> p g t i", i=RUN, t=SLOTS),
+                source[:].rearrange("p (t g i) -> p g t i", i=RUN, t=SLOTS)[:, first // RUN : (first + count) // RUN],
             )
 
         def weave_pair(copy, c, first):
@@ -133,15 +135,20 @@ def tile_picked_sidegate_silu_l_kernel(tc, xT, side, w1_words, w1_scales, offs, 
             nc.sync.dma_start(out=side_rows[i][:], in_=side[P * i : P * (i + 1), :])
             nc.sync.dma_start(out=w_codes[i][:].bitcast(I32), in_=w1_words[i].bitcast(I32))
 
-        for pair in (0, 2):
-            for entries in halves:
-                gather_plane("vector", pair, entries)
-                gather_plane("scalar", pair + 1, entries)
-            weave_pair(nc.vector.tensor_copy, 0, pair)
-            weave_pair(nc.scalar.copy if pair == 0 else nc.vector.tensor_copy, 1, pair)
-            if pair == 0:
-                for z in range(PASSES):
-                    nc.vector.tensor_copy(w_scales[64:128, z, 0, :].bitcast(I32), w_scales[0:64, z, 1, :].bitcast(I32))
+        gather_plane("vector", 0, halves[0])
+        gather_plane("scalar", 1, halves[0])
+        gather_plane("vector", 0, quarters[2])
+        gather_plane("scalar", 1, halves[1])
+        gather_plane("scalar", 0, quarters[3])
+        weave_pair(nc.vector.tensor_copy, 0, 0)
+        for z in range(PASSES):
+            nc.vector.tensor_copy(w_scales[64:128, z, 0, :].bitcast(I32), w_scales[0:64, z, 1, :].bitcast(I32))
+        for entries in halves:
+            gather_plane("vector", 2, entries)
+            gather_plane("scalar", 3, entries)
+        weave_pair(nc.vector.tensor_copy, 0, 2)
+        weave_four(nc.vector.tensor_copy, 0, slice(HALF, S - SCALAR_WEAVES))
+        weave_four(nc.scalar.copy, 0, slice(S - SCALAR_WEAVES, S))
         for c in range(2):
             quantise(0, c)
         for m in range(ROW_TILES):
@@ -154,9 +161,9 @@ def tile_picked_sidegate_silu_l_kernel(tc, xT, side, w1_words, w1_scales, offs, 
         for c in range(2):
             gather_plane("vector", 7, quarters[2 * c])
             gather_plane("scalar", 7, quarters[2 * c + 1])
-        weave_four(nc.vector.tensor_copy, slice(0, HALF - SCALAR_WEAVES))
-        weave_four(nc.scalar.copy, slice(HALF - SCALAR_WEAVES, HALF))
-        weave_four(nc.vector.tensor_copy, halves[1])
+        weave_four(nc.vector.tensor_copy, 1, slice(0, HALF - SCALAR_WEAVES))
+        weave_four(nc.scalar.copy, 1, slice(HALF - SCALAR_WEAVES, HALF))
+        weave_four(nc.vector.tensor_copy, 1, halves[1])
         for c in range(2):
             quantise(1, c)
         for m in range(ROW_TILES):

from contextlib import ExitStack

import concourse.mybir as mybir

K, T, S, N = 1024, 1024, 512, 256
FLOPS = 2 * K * N * S

F32 = mybir.dt.float32
BF16 = mybir.dt.bfloat16
I32 = mybir.dt.int32
U32 = mybir.dt.uint32
U16 = mybir.dt.uint16
U8 = mybir.dt.uint8
FP8X4 = mybir.dt.float8_e4m3fn_x4
FP4X4 = mybir.dt.float4_e2m1fn_x4
COPY = mybir.ActivationFunctionType.Copy
SILU = mybir.ActivationFunctionType.Silu
MULT = mybir.AluOpType.mult

P = 128
SLOTS = 4
K_PASS = P * SLOTS
PASSES = K // K_PASS
ROW_TILES = N // P
HALF = S // 2
QUARTER = S // 4
X_LOADS = ((0, 2), (2, 2), (4, 2), (6, 1), (7, 1))
SCALAR_SHARE_SIDE_1 = 128
SCALAR_WEAVES = 64
VECTOR_SHARE_PLANE_5 = 256
VECTOR_SHARE_PLANE_6 = 352
RUN = 4


def tile_picked_sidegate_silu_l_kernel(tc, xT, side, w1_words, w1_scales, offs, out):
    nc = tc.nc
    with ExitStack() as ctx:
        keep = ctx.enter_context(tc.tile_pool(name="keep", bufs=1))
        psum = ctx.enter_context(tc.psum_pool(name="psum", bufs=1))

        halves = [slice(HALF * c, HALF * (c + 1)) for c in range(2)]
        quarters = [slice(QUARTER * i, QUARTER * (i + 1)) for i in range(4)]
        offsets = keep.tile([P, S // 16], U16, name="offsets")
        w_codes = [keep.tile([P, 2 * N], U8, name=f"w_codes{z}", align_bytes=256) for z in range(PASSES)]
        w_scales = keep.tile([P, PASSES, 2, N], U8, name="w_scales", align_bytes=256)
        x_rows = [keep.tile([P, count * T], F32, name=f"x_rows{plane}", align_bytes=256) for plane, count in X_LOADS]
        planes = [rows[:, T * i : T * (i + 1)] for rows, load in zip(x_rows, X_LOADS) for i in range(load[1])]
        picked0 = [keep.tile([P, SLOTS * HALF], F32, name=f"picked0_{c}", align_bytes=64) for c in range(2)]
        picked1 = keep.tile([P, SLOTS * S], F32, name="picked1", align_bytes=64)
        woven = [[keep.tile([P, SLOTS * HALF], BF16, name=f"woven{z}_{c}", align_bytes=64) for c in range(2)] for z in range(PASSES)]
        x_codes = [keep.tile([P, S], U32, name=f"x_codes{z}", align_bytes=64) for z in range(PASSES)]
        x_scales = [keep.tile([P, S], U8, name=f"x_scales{z}", align_bytes=64) for z in range(PASSES)]
        side_rows = [keep.tile([P, T], F32, name=f"side_rows{m}", align_bytes=256) for m in range(ROW_TILES)]
        side_picked = [keep.tile([P, S], F32, name=f"side_picked{m}", align_bytes=64) for m in range(ROW_TILES)]
        gate = [keep.tile([P, S], F32, name=f"gate{m}", align_bytes=64) for m in range(ROW_TILES)]
        result = [keep.tile([P, S], F32, name=f"result{m}", align_bytes=256) for m in range(ROW_TILES)]
        acc = [[psum.tile([P, HALF], F32, name=f"acc{m}_{c}") for c in range(2)] for m in range(ROW_TILES)]

        def listed(window, entries):
            return window.indirect(offsets[:, entries.start // 16 : entries.stop // 16])

        def gather(engine, dst, window, entries):
            if engine == "vector":
                nc.vector.tensor_copy(dst, listed(window, entries))
            else:
                nc.scalar.activation(dst, listed(window, entries), COPY)

        def gather_plane(engine, plane, entries):
            z, t = divmod(plane, SLOTS)
            if z == 0:
                c, start = divmod(entries.start, HALF)
                dst = picked0[c][:, HALF * t + start : HALF * t + start + entries.stop - entries.start]
            else:
                dst = picked1[:, S * t + entries.start : S * t + entries.stop]
            gather(engine, dst, planes[plane], entries)

        def gather_side(engine, m, entries):
            gather(engine, side_picked[m][:, entries], side_rows[m][:], entries)

        def weave_four(copy, z, entries):
            c, start = divmod(entries.start, HALF)
            count = entries.stop - entries.start
            source, first = (picked1, entries.start) if z == 1 else (picked0[c], start)
            copy(
                woven[z][c][:, SLOTS * start : SLOTS * (start + count)].rearrange("p (g i t) -> p g t i", i=RUN, t=SLOTS),
                source[:].rearrange("p (t g i) -> p g t i", i=RUN, t=SLOTS)[:, first // RUN : (first + count) // RUN],
            )

        def weave_pair(copy, c, first):
            slots = woven[0][c][:].rearrange("p (j t) -> p j t", t=SLOTS)[:, :, first : first + 2]
            pair = picked0[c][:, HALF * first : HALF * (first + 2)]
            copy(slots, pair.rearrange("p (t j) -> p j t", t=2))

        def quantise(z, c):
            nc.vector.quantize_mx(
                out=x_codes[z][:, halves[c]].bitcast(FP8X4), scales=x_scales[z][:, halves[c]], in_=woven[z][c][:]
            )

        def multiply(z, m):
            for c in range(2):
                nc.tensor.matmul_mx(
                    out=acc[m][c][:],
                    lhsT=w_codes[z][:, 2 * P * m : 2 * P * (m + 1)].bitcast(FP4X4),
                    lhsT_scale=w_scales[:, z, 0, P * m : P * (m + 1)],
                    rhs=x_codes[z][:, halves[c]].bitcast(FP8X4),
                    rhs_scale=x_scales[z][:, halves[c]],
                    start=(z == 0),
                    stop=(z == PASSES - 1),
                )

        def silu(m, c):
            nc.scalar.activation(gate[m][:, halves[c]], side_picked[m][:, halves[c]], SILU)

        def finish(m, c):
            nc.vector.tensor_tensor(result[m][:, halves[c]], acc[m][c][:], gate[m][:, halves[c]], MULT)
            nc.sync.dma_start(out=out[P * m : P * (m + 1), halves[c]], in_=result[m][:, halves[c]])

        nc.vector.memset(w_scales[:].rearrange("p z h c -> p (z h c)").bitcast(I32), 0)
        warm = keep.tile([P, 2], F32, name="warm")
        nc.vector.memset(warm[:, 0:1], 0.0)
        nc.scalar.activation(warm[:, 1:2], warm[:, 0:1], SILU)

        for (plane, count), loaded in zip(X_LOADS, x_rows):
            z, t = divmod(plane, SLOTS)
            rows = xT[K_PASS * z : K_PASS * (z + 1), :].rearrange("(p t) w -> p (t w)", t=SLOTS)
            nc.sync.dma_start(out=loaded[:], in_=rows[:, T * t : T * (t + count)])
            if plane == 0:
                nc.sync.dma_start(offsets[:], offs)
                for q in range(2):
                    nc.sync.dma_start(
                        out=w_scales[32 * q : 32 * q + 4].rearrange("r z h c -> r (z h) c").bitcast(I32),
                        in_=w1_scales.rearrange("z (h q r) c -> q r (z h) c", h=2, q=2)[q].bitcast(I32),
                    )
        for i in range(2):
            nc.sync.dma_start(out=side_rows[i][:], in_=side[P * i : P * (i + 1), :])
            nc.sync.dma_start(out=w_codes[i][:].bitcast(I32), in_=w1_words[i].bitcast(I32))

        gather_plane("vector", 0, halves[0])
        gather_plane("scalar", 1, halves[0])
        gather_plane("vector", 0, quarters[2])
        gather_plane("scalar", 1, halves[1])
        gather_plane("scalar", 0, quarters[3])
        weave_pair(nc.vector.tensor_copy, 0, 0)
        for z in range(PASSES):
            nc.vector.tensor_copy(w_scales[64:128, z, 0, :].bitcast(I32), w_scales[0:64, z, 1, :].bitcast(I32))
        for entries in halves:
            gather_plane("vector", 2, entries)
            gather_plane("scalar", 3, entries)
        weave_pair(nc.vector.tensor_copy, 0, 2)
        weave_four(nc.vector.tensor_copy, 0, slice(HALF, S - SCALAR_WEAVES))
        weave_four(nc.scalar.copy, 0, slice(S - SCALAR_WEAVES, S))
        for c in range(2):
            quantise(0, c)
        for m in range(ROW_TILES):
            multiply(0, m)

        gather_plane("scalar", 4, slice(0, S))
        for plane, share in ((5, VECTOR_SHARE_PLANE_5), (6, VECTOR_SHARE_PLANE_6)):
            gather_plane("vector", plane, slice(0, share))
            gather_plane("scalar", plane, slice(share, S))
        for c in range(2):
            gather_plane("vector", 7, quarters[2 * c])
            gather_plane("scalar", 7, quarters[2 * c + 1])
        weave_four(nc.vector.tensor_copy, 1, slice(0, HALF - SCALAR_WEAVES))
        weave_four(nc.scalar.copy, 1, slice(HALF - SCALAR_WEAVES, HALF))
        weave_four(nc.vector.tensor_copy, 1, halves[1])
        for c in range(2):
            quantise(1, c)
        for m in range(ROW_TILES):
            multiply(1, m)

        for entries in halves:
            gather_side("scalar", 0, entries)
        cut = S - SCALAR_SHARE_SIDE_1
        gather_side("vector", 1, halves[0])
        gather_side("vector", 1, slice(HALF, cut))
        for c in range(2):
            silu(0, c)
        gather_side("scalar", 1, slice(cut, S))
        for c in range(2):
            silu(1, c)
        for m in range(ROW_TILES):
            for c in range(2):
                finish(m, c)
